import numpy as np
import ml_dtypes


def mxq(x, axis, fmt="e4m3"):
    dtype, down = {"e4m3": (ml_dtypes.float8_e4m3fn, 7), "e5m2": (ml_dtypes.float8_e5m2, 14)}[fmt]
    v = np.moveaxis(np.asarray(x, np.float32).astype(ml_dtypes.bfloat16).astype(np.float64), axis, -1)
    blocks = v.reshape(v.shape[:-1] + (-1, 32))
    amax = np.abs(blocks).max(-1, keepdims=True)
    byte = np.maximum(np.where(amax > 0, np.frexp(amax)[1] - 1 + 127, 0) - down, 1)
    scale = np.exp2(byte - 127.0)
    codes = (blocks / scale).astype(np.float32).astype(dtype).astype(np.float64)
    return np.moveaxis((codes * scale).reshape(v.shape), -1, axis)


WIDE = False


def mx_kscale(k):
    if not WIDE:
        return np.ones(k)
    levels = np.array([30, -30])
    if k % 512:
        return np.exp2(np.random.permutation(np.resize(levels, k // 32))).repeat(32)
    a = np.empty((k // 512, 16))
    for p in range(k // 512):
        a[p, :8] = np.random.permutation(np.resize(levels, 8))
        for g in range(8):
            far = levels[np.abs(levels - a[p, g]) >= 10]
            a[p, g + 8] = far[np.random.randint(len(far))]
    return np.exp2(a.ravel()).repeat(32)


BF16 = ml_dtypes.bfloat16


def bf(x):
    return np.asarray(x, np.float32).astype(BF16)


def f64(x):
    return np.asarray(x).astype(np.float64)


E2M1 = np.array([0.0, 0.5, 1.0, 1.5, 2.0, 3.0, 4.0, 6.0, -0.0, -0.5, -1.0, -1.5, -2.0, -3.0, -4.0, -6.0])


def pack_weight(w, fmt):
    k, n = w.shape
    w = f64(bf(w)).reshape(k // 32, 32, n)
    amax = np.abs(w).max(1)
    if fmt == "e4m3":
        byte = np.frexp(amax)[1] - 1 + 127 - 7
    else:
        mant, ex = np.frexp(amax / 6.0)
        byte = np.where(mant > 0.5, ex, ex - 1) + 127
    byte = np.clip(np.where(amax > 0, byte, 1), 1, 254)
    scaled = (w * np.exp2(127.0 - byte)[:, None, :]).reshape(k, n).astype(np.float32)
    by_word = np.ascontiguousarray(scaled.reshape(k // 512, 128, 4, n).transpose(0, 1, 3, 2))
    if fmt == "e4m3":
        words = by_word.astype(ml_dtypes.float8_e4m3fn).view(np.uint8)
    else:
        c = by_word.astype(ml_dtypes.float4_e2m1fn).view(np.uint8) & 0xF
        words = c[..., 0::2] | (c[..., 1::2] << 4)
    return np.ascontiguousarray(words), np.ascontiguousarray(byte.astype(np.uint8).reshape(k // 512, 16, n))


def unpack_weight(words, scales, fmt):
    g, p, n, _ = words.shape
    if fmt == "e4m3":
        vals = np.ascontiguousarray(words).view(ml_dtypes.float8_e4m3fn).astype(np.float64)
    else:
        nib = np.empty((g, p, n, 4), np.uint8)
        nib[..., 0::2] = words & 0xF
        nib[..., 1::2] = words >> 4
        vals = E2M1[nib]
    vals = vals * np.repeat(np.exp2(scales.astype(np.float64) - 127.0), 8, axis=1)[..., None]
    return vals.transpose(0, 1, 3, 2).reshape(g * 512, n)
def pack4(w):
    words, scales = pack_weight(w, "e2m1")
    return words.reshape(words.shape[0], 128, -1), scales


def unpack4(words, scales):
    return unpack_weight(words.reshape(words.shape[0], 128, -1, 2), scales, "e2m1")


K, B = 2048, 512


def setup_inputs():
    s = mx_kscale(K)
    operator = np.random.standard_normal((K, K)) / np.sqrt(K) / s[:, None] / s
    a_words, a_scales = pack4(operator)
    return {"dirs": bf(np.random.standard_normal((K, B)) * K ** -0.25 * s[:, None]),
            "a_words": a_words,
            "a_scales": a_scales,
            "pot": bf(0.5 * np.random.standard_normal(K) / (s * s)),
            "rho": bf(1 + 0.1 * np.random.standard_normal(B))}


def reference(dirs, a_words, a_scales, pot, rho):
    d = f64(dirs)
    r = f64(rho)
    dq = mxq(d, 0, "e4m3")
    a = unpack4(a_words, a_scales)
    applied = a.T @ dq
    w = applied + f64(pot)[:, None] * d
    h = dq.T @ mxq(w, 0, "e5m2")
    return h * r[:, None] * r

@@ -1,0 +1,260 @@
+from contextlib import ExitStack
+
+import concourse.mybir as mybir
+from concourse.masks import make_identity
+
+K, B = 2048, 512
+FLOPS = 2 * K * K * B + 2 * K * B * B
+
+F32 = mybir.dt.float32
+BF16 = mybir.dt.bfloat16
+U32 = mybir.dt.uint32
+I32 = mybir.dt.int32
+U8 = mybir.dt.uint8
+E4M3X4 = mybir.dt.float8_e4m3fn_x4
+E5M2X4 = mybir.dt.float8_e5m2_x4
+E2M1X4 = mybir.dt.float4_e2m1fn_x4
+MULT = mybir.AluOpType.mult
+ADD = mybir.AluOpType.add
+
+P = 128
+GROUPS = K // 512
+V_COLS = 320
+
+
+def interleaved(tile_ap):
+    return tile_ap.rearrange("p (c i) t -> p c t i", i=4)
+
+
+def by_row(tile_ap):
+    return tile_ap.rearrange("p t (c i) -> p c t i", i=4)
+
+
+def tile_scaled_block_projection_s9_kernel(tc, dirs, a_words, a_scales, pot, rho, out):
+    nc = tc.nc
+    with ExitStack() as ctx:
+        keep = ctx.enter_context(tc.tile_pool(name="keep", bufs=1))
+        psum = ctx.enter_context(tc.psum_pool(name="psum", bufs=1))
+        ctx.enter_context(tc.manual_schedule())
+
+        def sb(shape, dtype, name):
+            return keep.tile(shape, dtype, name=name, tag=name, align_bytes=64)
+
+        def bank(i, dtype=F32, cols=512):
+            return psum.tile([P, cols], dtype, name="bank%d" % i, tag="bank%d" % i)
+
+        G = range(GROUPS)
+        d_raw = [sb([P, 4, B], BF16, "d_raw%d" % g) for g in G]
+        d_int = [sb([P, B, 4], BF16, "d_int%d" % g) for g in G]
+        d_codes = [sb([P, B], U32, "d_codes%d" % g) for g in G]
+        d_scales = [sb([P, B], U8, "d_scales%d" % g) for g in G]
+        e_raw = [sb([P, 4, B], BF16, "e_raw%d" % g) for g in G]
+        e_int = [sb([P, B, 4], BF16, "e_int%d" % g) for g in G]
+        e_codes = [sb([P, B], U32, "e_codes%d" % g) for g in G]
+        e_scales = [sb([P, B], U8, "e_scales%d" % g) for g in G]
+        w_raw = [sb([P, 4, B], BF16, "w_raw%d" % g) for g in G]
+        w_int = [sb([P, B, 4], BF16, "w_int%d" % g) for g in G]
+        w_codes = [sb([P, B], U32, "w_codes%d" % g) for g in G]
+        w_scales = [sb([P, B], U8, "w_scales%d" % g) for g in G]
+        a_raw = [sb([P, 2 * K], U8, "a_raw%d" % g) for g in G]
+        a_perm = [sb([P, 2 * K], U8, "a_perm%d" % g) for g in G]
+        s_raw = [sb([P, GROUPS, K // 2], U8, "s_raw%d" % h) for h in range(2)]
+        s_perm = [sb([P, GROUPS, K // 2], U8, "s_perm%d" % h) for h in range(2)]
+        rows = sb([P, P], BF16, "rows")
+        ident = sb([P, P], BF16, "ident")
+        coef = sb([P, 20], F32, "coef")
+        rho_all = sb([P, B], BF16, "rho_all")
+
+        def load_scales(h):
+            for q in range(4):
+                nc.sync.dma_start(
+                    out=s_raw[h][32 * q : 32 * q + 4, :, :].bitcast(I32),
+                    in_=a_scales[:, 4 * q : 4 * q + 4, 1024 * h : 1024 * (h + 1)]
+                    .rearrange("g r n -> r g n")
+                    .bitcast(I32),
+                )
+
+        def load_a(g, lo, hi):
+            nc.sync.dma_start(
+                out=a_raw[g][:, 2 * lo : 2 * hi].bitcast(I32),
+                in_=a_words[g][:, 2 * lo : 2 * hi].bitcast(I32),
+            )
+
+        def load_e(g):
+            src = dirs[512 * g : 512 * (g + 1), :].rearrange("(s t r) b -> r s t b", t=4, r=4)
+            for r in range(4):
+                nc.sync.dma_start(out=e_raw[g][r : 128 : 4, :, :], in_=src[r])
+
+        for h in range(2):
+            nc.vector.memset(s_raw[h][:].rearrange("p g n -> p (g n)").bitcast(I32), 0)
+        nc.gpsimd.memset(rows[:], 0.0)
+        make_identity(nc, ident[:])
+        for g in G:
+            nc.sync.dma_start(
+                out=d_raw[g][:],
+                in_=dirs[512 * g : 512 * (g + 1), :].rearrange("(p t) b -> p t b", t=4),
+            )
+            if g == 0:
+                load_scales(0)
+            load_a(g, 0, 1024)
+        load_e(0)
+        load_scales(1)
+        for g in G:
+            load_a(g, 1024, 1536)
+        load_e(1)
+        for g in G:
+            load_a(g, 1536, 2048)
+        load_e(2)
+        load_e(3)
+        nc.sync.dma_start(out=rho_all[:], in_=rho.partition_broadcast(P))
+
+        for g in G:
+            nc.gpsimd.dma_start(
+                out=rows[4 * g : 4 * g + 4, :].rearrange("t (s r) -> t s r", r=4),
+                in_=pot[512 * g : 512 * (g + 1)].rearrange("(s t r) -> t s r", t=4, r=4),
+            )
+        nc.gpsimd.dma_start(out=rows[16:20, :], in_=rho.rearrange("(m x) -> m x", x=P))
+
+        def perm_scales(h):
+            nc.vector.tensor_copy(
+                out=s_perm[h][:].rearrange("p g n -> p (g n)").bitcast(I32).rearrange("p (x t s) -> p x t s", t=4, s=32),
+                in_=s_raw[h][:].rearrange("p g n -> p (g n)").bitcast(I32).rearrange("p (x s t) -> p x t s", t=4, s=32),
+            )
+
+        def perm_words(g, jg):
+            cols = slice(1024 * jg, 1024 * (jg + 1))
+            nc.vector.tensor_copy(
+                out=a_perm[g][:, cols].bitcast(I32).rearrange("p (t s e) -> p t s e", t=4, e=2),
+                in_=a_raw[g][:, cols].bitcast(I32).rearrange("p (s t e) -> p t s e", t=4, e=2),
+            )
+
+        def v_interleave(dst, src, lo, hi):
+            nc.vector.tensor_copy(out=interleaved(dst[:, lo:hi, :]), in_=by_row(src[:, :, lo:hi]))
+
+        def s_interleave(dst, src, lo, hi):
+            nc.scalar.copy(out=interleaved(dst[:, lo:hi, :]), in_=by_row(src[:, :, lo:hi]))
+
+        def g_interleave(dst, src, lo, hi):
+            nc.gpsimd.tensor_scalar(
+                out=interleaved(dst[:, lo:hi, :]), in0=by_row(src[:, :, lo:hi]),
+                scalar1=1.0, scalar2=0.0, op0=MULT, op1=ADD,
+            )
+
+        def quantize(codes, scales, src, fmt):
+            nc.vector.quantize_mx(
+                out=codes[:].bitcast(fmt), scales=scales[:], in_=src[:].rearrange("p b t -> p (b t)")
+            )
+
+        def mm1(acc, g, i):
+            h, n = divmod(i, 8)
+            nc.tensor.matmul_mx(
+                out=acc[:],
+                lhsT=a_perm[g][:, 256 * i : 256 * (i + 1)].bitcast(E2M1X4),
+                lhsT_scale=s_perm[h][:, g, 128 * n : 128 * (n + 1)],
+                rhs=d_codes[g][:].bitcast(E4M3X4),
+                rhs_scale=d_scales[g][:],
+                start=(g == 0),
+                stop=(g == GROUPS - 1),
+            )
+
+        def combine(acc, i):
+            jg, t = divmod(i, 4)
+            nc.vector.scalar_tensor_tensor(
+                out=w_raw[jg][:, t, :], in0=e_raw[jg][:, t, :], scalar=coef[:, i : i + 1],
+                in1=acc[:], op0=MULT, op1=ADD,
+            )
+
+        def mm2(acc, jg, m):
+            cols = slice(128 * m, 128 * (m + 1))
+            nc.tensor.matmul_mx(
+                out=acc[:],
+                lhsT=e_codes[jg][:, cols].bitcast(E4M3X4),
+                lhsT_scale=e_scales[jg][:, cols],
+                rhs=w_codes[jg][:].bitcast(E5M2X4),
+                rhs_scale=w_scales[jg][:],
+                start=(jg == 0),
+                stop=(jg == GROUPS - 1),
+            )
+
+        turned = bank(7, BF16, P)
+        acc = [None] * 16
+        for i in range(7):
+            acc[i] = bank(i)
+        for g in G:
+            v_interleave(d_int[g], d_raw[g], 0, V_COLS)
+            s_interleave(d_int[g], d_raw[g], V_COLS, B)
+            if g == 0:
+                perm_scales(0)
+            perm_words(g, 0)
+            quantize(d_codes[g], d_scales[g], d_int[g], E4M3X4)
+            perm_words(g, 1)
+            for i in range(7):
+                mm1(acc[i], g, i)
+            if g == 1:
+                nc.tensor.transpose(turned[:], rows[:], ident[:])
+            if g == 2:
+                nc.scalar.copy(out=coef[:], in_=turned[:, 0:20])
+        acc[7] = bank(7)
+        for g in G:
+            mm1(acc[7], g, 7)
+
+        s_interleave(e_int[0], e_raw[0], 0, B)
+        g_interleave(e_int[2], e_raw[2], 0, B)
+        g_interleave(e_int[3], e_raw[3], 0, B)
+
+        combine(acc[0], 0)
+        combine(acc[1], 1)
+        perm_scales(1)
+        for g in G:
+            perm_words(g, 2)
+        combine(acc[2], 2)
+        combine(acc[3], 3)
+        s_interleave(w_int[0], w_raw[0], 0, B)
+        quantize(e_codes[0], e_scales[0], e_int[0], E4M3X4)
+        for i in range(8, 12):
+            acc[i] = bank(i - 8)
+            for g in G:
+                mm1(acc[i], g, i)
+        combine(acc[4], 4)
+        combine(acc[5], 5)
+        for g in G:
+            perm_words(g, 3)
+        combine(acc[6], 6)
+        combine(acc[7], 7)
+        s_interleave(e_int[1], e_raw[1], 0, B)
+        s_interleave(w_int[1], w_raw[1], 0, B)
+        for i in range(12, 16):
+            acc[i] = bank(i - 8)
+            for g in G:
+                mm1(acc[i], g, i)
+        combine(acc[8], 8)
+        quantize(w_codes[0], w_scales[0], w_int[0], E5M2X4)
+        combine(acc[9], 9)
+        quantize(e_codes[1], e_scales[1], e_int[1], E4M3X4)
+        combine(acc[10], 10)
+        combine(acc[11], 11)
+        s_interleave(w_int[2], w_raw[2], 0, B)
+        quantize(e_codes[2], e_scales[2], e_int[2], E4M3X4)
+        h_acc = [bank(m) for m in range(4)]
+        for m in range(4):
+            mm2(h_acc[m], 0, m)
+        combine(acc[12], 12)
+        quantize(w_codes[1], w_scales[1], w_int[1], E5M2X4)
+        for m in range(4):
+            mm2(h_acc[m], 1, m)
+        combine(acc[13], 13)
+        combine(acc[14], 14)
+        combine(acc[15], 15)
+        quantize(e_codes[3], e_scales[3], e_int[3], E4M3X4)
+        v_interleave(w_int[3], w_raw[3], 0, V_COLS)
+        s_interleave(w_int[3], w_raw[3], V_COLS, B)
+        quantize(w_codes[2], w_scales[2], w_int[2], E5M2X4)
+        quantize(w_codes[3], w_scales[3], w_int[3], E5M2X4)
+        for jg, m in ((2, 0), (2, 1), (3, 0), (2, 2), (3, 1), (2, 3), (3, 2), (3, 3)):
+            mm2(h_acc[m], jg, m)
+        for m in range(4):
+            res = sb([P, B], F32, "res%d" % m)
+            nc.vector.scalar_tensor_tensor(
+                out=res[:], in0=h_acc[m][:], scalar=coef[:, 16 + m : 17 + m], in1=rho_all[:], op0=MULT, op1=MULT,
+            )
+            nc.sync.dma_start(out=out[128 * m : 128 * (m + 1), :], in_=res[:])

@@ -19,7 +19,6 @@ ADD = mybir.AluOpType.add
 
 P = 128
 GROUPS = K // 512
-V_COLS = 320
 
 
 def interleaved(tile_ap):
@@ -48,18 +47,20 @@ def tile_scaled_block_projection_s9_kernel(tc, dirs, a_words, a_scales, pot, rho
         d_int = [sb([P, B, 4], BF16, "d_int%d" % g) for g in G]
         d_codes = [sb([P, B], U32, "d_codes%d" % g) for g in G]
         d_scales = [sb([P, B], U8, "d_scales%d" % g) for g in G]
+        FLAT = ()
         e_raw = [sb([P, 4, B], BF16, "e_raw%d" % g) for g in G]
-        e_int = [sb([P, B, 4], BF16, "e_int%d" % g) for g in G]
-        e_codes = [sb([P, B], U32, "e_codes%d" % g) for g in G]
-        e_scales = [sb([P, B], U8, "e_scales%d" % g) for g in G]
+        e_int = [None if g in FLAT else sb([P, B, 4], BF16, "e_int%d" % g) for g in G]
+        e_codes = [d_codes[g] if g in FLAT else sb([P, B], U32, "e_codes%d" % g) for g in G]
+        e_scales = [d_scales[g] if g in FLAT else sb([P, B], U8, "e_scales%d" % g) for g in G]
+        a_perm = [[None if j in FLAT else sb([P, 1024], U8, "a_perm%d_%d" % (g, j)) for j in G] for g in G]
+        s_perm = [None if j in FLAT else sb([P, GROUPS, B], U8, "s_perm%d" % j) for j in G]
+        w_flat = [sb([P, B], BF16, "w_flat%d" % i) for i in range(4 * len(FLAT))]
         w_raw = [sb([P, 4, B], BF16, "w_raw%d" % g) for g in G]
         w_int = [sb([P, B, 4], BF16, "w_int%d" % g) for g in G]
         w_codes = [sb([P, B], U32, "w_codes%d" % g) for g in G]
         w_scales = [sb([P, B], U8, "w_scales%d" % g) for g in G]
         a_raw = [sb([P, 2 * K], U8, "a_raw%d" % g) for g in G]
-        a_perm = [sb([P, 2 * K], U8, "a_perm%d" % g) for g in G]
         s_raw = [sb([P, GROUPS, K // 2], U8, "s_raw%d" % h) for h in range(2)]
-        s_perm = [sb([P, GROUPS, K // 2], U8, "s_perm%d" % h) for h in range(2)]
         rows = sb([P, P], BF16, "rows")
         ident = sb([P, P], BF16, "ident")
         coef = sb([P, 20], F32, "coef")
@@ -80,53 +81,46 @@ def tile_scaled_block_projection_s9_kernel(tc, dirs, a_words, a_scales, pot, rho
                 in_=a_words[g][:, 2 * lo : 2 * hi].bitcast(I32),
             )
 
+        def load_d(g):
+            nc.sync.dma_start(
+                out=d_raw[g][:],
+                in_=dirs[512 * g : 512 * (g + 1), :].rearrange("(p t) b -> p t b", t=4),
+            )
+
         def load_e(g):
-            src = dirs[512 * g : 512 * (g + 1), :].rearrange("(s t r) b -> r s t b", t=4, r=4)
-            for r in range(4):
-                nc.sync.dma_start(out=e_raw[g][r : 128 : 4, :, :], in_=src[r])
+            src = dirs[512 * g : 512 * (g + 1), :]
+            if g in FLAT:
+                nc.sync.dma_start(out=e_raw[g][:], in_=src.rearrange("(m p) b -> p m b", m=4))
+            else:
+                quads = src.rearrange("(s t r) b -> r s t b", t=4, r=4)
+                for r in range(4):
+                    nc.sync.dma_start(out=e_raw[g][r : 128 : 4, :, :], in_=quads[r])
+
+        def load_rows():
+            for g in range(len(FLAT), GROUPS):
+                nc.gpsimd.dma_start(
+                    out=rows[4 * g : 4 * g + 4, :].rearrange("t (s r) -> t s r", r=4),
+                    in_=pot[512 * g : 512 * (g + 1)].rearrange("(s t r) -> t s r", t=4, r=4),
+                )
+            nc.gpsimd.dma_start(out=rows[16:20, :], in_=rho.rearrange("(m x) -> m x", x=P))
+
+        def perm_scales(j):
+            h, k = divmod(j, 2)
+            nc.vector.tensor_copy(
+                out=s_perm[j][:].bitcast(I32).rearrange("p g (t s) -> p g t s", t=4),
+                in_=s_raw[h][:, :, 512 * k : 512 * (k + 1)].bitcast(I32).rearrange("p g (s t) -> p g t s", t=4),
+            )
+
+        def perm_words(g, j):
+            nc.vector.tensor_copy(
+                out=a_perm[g][j][:].bitcast(I32).rearrange("p (t s e) -> p t s e", t=4, e=2),
+                in_=a_raw[g][:, 1024 * j : 1024 * (j + 1)].bitcast(I32).rearrange("p (s t e) -> p t s e", t=4, e=2),
+            )
 
         for h in range(2):
             nc.vector.memset(s_raw[h][:].rearrange("p g n -> p (g n)").bitcast(I32), 0)
         nc.gpsimd.memset(rows[:], 0.0)
         make_identity(nc, ident[:])
-        for g in G:
-            nc.sync.dma_start(
-                out=d_raw[g][:],
-                in_=dirs[512 * g : 512 * (g + 1), :].rearrange("(p t) b -> p t b", t=4),
-            )
-            if g == 0:
-                load_scales(0)
-            load_a(g, 0, 1024)
-        load_e(0)
-        load_scales(1)
-        for g in G:
-            load_a(g, 1024, 1536)
-        load_e(1)
-        for g in G:
-            load_a(g, 1536, 2048)
-        load_e(2)
-        load_e(3)
-        nc.sync.dma_start(out=rho_all[:], in_=rho.partition_broadcast(P))
-
-        for g in G:
-            nc.gpsimd.dma_start(
-                out=rows[4 * g : 4 * g + 4, :].rearrange("t (s r) -> t s r", r=4),
-                in_=pot[512 * g : 512 * (g + 1)].rearrange("(s t r) -> t s r", t=4, r=4),
-            )
-        nc.gpsimd.dma_start(out=rows[16:20, :], in_=rho.rearrange("(m x) -> m x", x=P))
-
-        def perm_scales(h):
-            nc.vector.tensor_copy(
-                out=s_perm[h][:].rearrange("p g n -> p (g n)").bitcast(I32).rearrange("p (x t s) -> p x t s", t=4, s=32),
-                in_=s_raw[h][:].rearrange("p g n -> p (g n)").bitcast(I32).rearrange("p (x s t) -> p x t s", t=4, s=32),
-            )
-
-        def perm_words(g, jg):
-            cols = slice(1024 * jg, 1024 * (jg + 1))
-            nc.vector.tensor_copy(
-                out=a_perm[g][:, cols].bitcast(I32).rearrange("p (t s e) -> p t s e", t=4, e=2),
-                in_=a_raw[g][:, cols].bitcast(I32).rearrange("p (s t e) -> p t s e", t=4, e=2),
-            )
 
         def v_interleave(dst, src, lo, hi):
             nc.vector.tensor_copy(out=interleaved(dst[:, lo:hi, :]), in_=by_row(src[:, :, lo:hi]))
@@ -134,127 +128,253 @@ def tile_scaled_block_projection_s9_kernel(tc, dirs, a_words, a_scales, pot, rho
         def s_interleave(dst, src, lo, hi):
             nc.scalar.copy(out=interleaved(dst[:, lo:hi, :]), in_=by_row(src[:, :, lo:hi]))
 
-        def g_interleave(dst, src, lo, hi):
-            nc.gpsimd.tensor_scalar(
-                out=interleaved(dst[:, lo:hi, :]), in0=by_row(src[:, :, lo:hi]),
-                scalar1=1.0, scalar2=0.0, op0=MULT, op1=ADD,
-            )
-
         def quantize(codes, scales, src, fmt):
             nc.vector.quantize_mx(
                 out=codes[:].bitcast(fmt), scales=scales[:], in_=src[:].rearrange("p b t -> p (b t)")
             )
 
         def mm1(acc, g, i):
-            h, n = divmod(i, 8)
+            j, n = divmod(i, 4)
+            if j in FLAT:
+                h = i // 8
+                words = a_raw[g][:, 256 * i : 256 * (i + 1)]
+                scales = s_raw[h][:, g, 128 * (i % 8) : 128 * (i % 8 + 1)]
+            else:
+                words = a_perm[g][j][:, 256 * n : 256 * (n + 1)]
+                scales = s_perm[j][:, g, 128 * n : 128 * (n + 1)]
             nc.tensor.matmul_mx(
                 out=acc[:],
-                lhsT=a_perm[g][:, 256 * i : 256 * (i + 1)].bitcast(E2M1X4),
-                lhsT_scale=s_perm[h][:, g, 128 * n : 128 * (n + 1)],
+                lhsT=words.bitcast(E2M1X4),
+                lhsT_scale=scales,
                 rhs=d_codes[g][:].bitcast(E4M3X4),
                 rhs_scale=d_scales[g][:],
                 start=(g == 0),
                 stop=(g == GROUPS - 1),
             )
 
-        def combine(acc, i):
-            jg, t = divmod(i, 4)
+        def combine(acc, i, queues):
+            j, n = divmod(i, 4)
             nc.vector.scalar_tensor_tensor(
-                out=w_raw[jg][:, t, :], in0=e_raw[jg][:, t, :], scalar=coef[:, i : i + 1],
+                out=w_flat[i][:] if j in FLAT else w_raw[j][:, n, :], in0=e_raw[j][:, n, :], scalar=coef[:, i : i + 1],
                 in1=acc[:], op0=MULT, op1=ADD,
             )
+            if j in FLAT:
+                for t in range(4):
+                    queues[t].dma_start(out=w_raw[j][32 * n : 32 * n + 32, t, :], in_=w_flat[i][t : 128 : 4, :])
 
-        def mm2(acc, jg, m):
+        def mm2(acc, j, m):
             cols = slice(128 * m, 128 * (m + 1))
             nc.tensor.matmul_mx(
                 out=acc[:],
-                lhsT=e_codes[jg][:, cols].bitcast(E4M3X4),
-                lhsT_scale=e_scales[jg][:, cols],
-                rhs=w_codes[jg][:].bitcast(E5M2X4),
-                rhs_scale=w_scales[jg][:],
-                start=(jg == 0),
-                stop=(jg == GROUPS - 1),
+                lhsT=e_codes[j][:, cols].bitcast(E4M3X4),
+                lhsT_scale=e_scales[j][:, cols],
+                rhs=w_codes[j][:].bitcast(E5M2X4),
+                rhs_scale=w_scales[j][:],
+                start=(j == 0),
+                stop=(j == GROUPS - 1),
             )
+
+        def finish(acc_m, m):
+            res = sb([P, B], F32, "res%d" % m)
+            nc.vector.scalar_tensor_tensor(
+                out=res[:], in0=acc_m[:], scalar=coef[:, 16 + m : 17 + m], in1=rho_all[:], op0=MULT, op1=MULT,
+            )
+            nc.sync.dma_start(out=out[128 * m : 128 * (m + 1), :], in_=res[:])
 
         turned = bank(7, BF16, P)
         acc = [None] * 16
-        for i in range(7):
-            acc[i] = bank(i)
-        for g in G:
-            v_interleave(d_int[g], d_raw[g], 0, V_COLS)
-            s_interleave(d_int[g], d_raw[g], V_COLS, B)
-            if g == 0:
-                perm_scales(0)
-            perm_words(g, 0)
-            quantize(d_codes[g], d_scales[g], d_int[g], E4M3X4)
-            perm_words(g, 1)
-            for i in range(7):
-                mm1(acc[i], g, i)
-            if g == 1:
-                nc.tensor.transpose(turned[:], rows[:], ident[:])
-            if g == 2:
-                nc.scalar.copy(out=coef[:], in_=turned[:, 0:20])
-        acc[7] = bank(7)
-        for g in G:
-            mm1(acc[7], g, 7)
-
-        s_interleave(e_int[0], e_raw[0], 0, B)
-        g_interleave(e_int[2], e_raw[2], 0, B)
-        g_interleave(e_int[3], e_raw[3], 0, B)
-
-        combine(acc[0], 0)
-        combine(acc[1], 1)
+        h_acc = [None] * 4
+        load_d(0)
+        load_a(0, 0, 1024)
+        load_scales(0)
+        load_a(1, 0, 1024)
+        load_d(1)
+        load_d(2)
+        v_interleave(d_int[0], d_raw[0], 0, 448)
+        s_interleave(d_int[0], d_raw[0], 448, 512)
+        load_d(3)
+        load_a(3, 0, 1024)
+        perm_words(0, 0)
+        load_rows()
+        quantize(d_codes[0], d_scales[0], d_int[0], E4M3X4)
+        load_a(2, 0, 1024)
+        perm_scales(0)
+        perm_words(0, 1)
+        acc[0] = bank(0)
+        mm1(acc[0], 0, 0)
+        perm_words(1, 0)
         perm_scales(1)
-        for g in G:
-            perm_words(g, 2)
-        combine(acc[2], 2)
-        combine(acc[3], 3)
-        s_interleave(w_int[0], w_raw[0], 0, B)
+        acc[1] = bank(1)
+        mm1(acc[1], 0, 1)
+        perm_words(1, 1)
+        acc[3] = bank(3)
+        mm1(acc[3], 0, 3)
+        v_interleave(d_int[1], d_raw[1], 0, 320)
+        s_interleave(d_int[1], d_raw[1], 320, 512)
+        acc[2] = bank(2)
+        mm1(acc[2], 0, 2)
+        acc[4] = bank(4)
+        mm1(acc[4], 0, 4)
+        acc[6] = bank(6)
+        mm1(acc[6], 0, 6)
+        quantize(d_codes[1], d_scales[1], d_int[1], E4M3X4)
+        load_e(0)
+        s_interleave(d_int[2], d_raw[2], 320, 512)
+        v_interleave(d_int[2], d_raw[2], 0, 320)
+        mm1(acc[3], 1, 3)
+        mm1(acc[6], 1, 6)
+        load_a(0, 1024, 2048)
+        s_interleave(d_int[3], d_raw[3], 192, 512)
+        mm1(acc[1], 1, 1)
+        v_interleave(d_int[3], d_raw[3], 0, 192)
+        mm1(acc[2], 1, 2)
+        nc.tensor.transpose(turned[:], rows[:], ident[:])
+        quantize(d_codes[2], d_scales[2], d_int[2], E4M3X4)
+        acc[5] = bank(5)
+        mm1(acc[5], 0, 5)
+        mm1(acc[0], 1, 0)
+        perm_words(2, 0)
+        perm_words(3, 0)
+        nc.scalar.copy(out=coef[:], in_=turned[:, 0:20])
+        mm1(acc[1], 2, 1)
+        quantize(d_codes[3], d_scales[3], d_int[3], E4M3X4)
+        load_e(1)
+        mm1(acc[0], 2, 0)
+        nc.sync.dma_start(out=rho_all[:], in_=rho.partition_broadcast(P))
+        mm1(acc[2], 2, 2)
+        perm_words(2, 1)
+        load_a(1, 1024, 2048)
+        mm1(acc[2], 3, 2)
+        perm_words(3, 1)
+        s_interleave(e_int[0], e_raw[0], 64, 512)
+        mm1(acc[6], 2, 6)
+        v_interleave(e_int[0], e_raw[0], 0, 64)
+        combine(acc[2], 2, (nc.sync, nc.sync, nc.sync, nc.sync))
+        mm1(acc[3], 2, 3)
+        acc[7] = bank(7)
+        mm1(acc[7], 0, 7)
+        perm_words(0, 2)
+        mm1(acc[1], 3, 1)
+        perm_words(0, 3)
+        mm1(acc[3], 3, 3)
+        combine(acc[1], 1, (nc.sync, nc.sync, nc.sync, nc.sync))
+        mm1(acc[0], 3, 0)
+        load_scales(1)
+        mm1(acc[4], 1, 4)
+        load_a(2, 1024, 2048)
+        combine(acc[0], 0, (nc.sync, nc.sync, nc.sync, nc.sync))
+        mm1(acc[5], 1, 5)
+        load_a(3, 1024, 2048)
+        s_interleave(e_int[1], e_raw[1], 0, 512)
+        mm1(acc[7], 1, 7)
+        combine(acc[3], 3, (nc.sync, nc.sync, nc.sync, nc.sync))
+        mm1(acc[5], 2, 5)
+        mm1(acc[7], 2, 7)
         quantize(e_codes[0], e_scales[0], e_int[0], E4M3X4)
-        for i in range(8, 12):
-            acc[i] = bank(i - 8)
-            for g in G:
-                mm1(acc[i], g, i)
-        combine(acc[4], 4)
-        combine(acc[5], 5)
-        for g in G:
-            perm_words(g, 3)
-        combine(acc[6], 6)
-        combine(acc[7], 7)
-        s_interleave(e_int[1], e_raw[1], 0, B)
-        s_interleave(w_int[1], w_raw[1], 0, B)
-        for i in range(12, 16):
-            acc[i] = bank(i - 8)
-            for g in G:
-                mm1(acc[i], g, i)
-        combine(acc[8], 8)
+        mm1(acc[7], 3, 7)
+        mm1(acc[5], 3, 5)
+        perm_words(1, 2)
+        mm1(acc[4], 2, 4)
+        combine(acc[7], 7, (nc.sync, nc.sync, nc.sync, nc.sync))
+        load_e(2)
+        mm1(acc[4], 3, 4)
+        mm1(acc[6], 3, 6)
+        combine(acc[5], 5, (nc.sync, nc.sync, nc.sync, nc.sync))
+        s_interleave(w_int[0], w_raw[0], 0, 512)
+        perm_scales(2)
+        combine(acc[4], 4, (nc.sync, nc.sync, nc.sync, nc.sync))
+        acc[9] = bank(1)
+        mm1(acc[9], 0, 9)
+        load_e(3)
+        acc[8] = bank(0)
+        mm1(acc[8], 0, 8)
+        combine(acc[6], 6, (nc.sync, nc.sync, nc.sync, nc.sync))
+        acc[10] = bank(2)
+        mm1(acc[10], 0, 10)
+        acc[11] = bank(3)
+        mm1(acc[11], 0, 11)
+        perm_words(2, 2)
+        mm1(acc[9], 1, 9)
+        perm_scales(3)
+        mm1(acc[8], 1, 8)
+        perm_words(2, 3)
+        mm1(acc[10], 1, 10)
+        s_interleave(w_int[1], w_raw[1], 0, 512)
+        perm_words(3, 2)
+        mm1(acc[11], 1, 11)
+        perm_words(1, 3)
+        mm1(acc[9], 2, 9)
+        perm_words(3, 3)
         quantize(w_codes[0], w_scales[0], w_int[0], E5M2X4)
-        combine(acc[9], 9)
+        mm1(acc[8], 2, 8)
+        mm1(acc[10], 2, 10)
+        mm1(acc[11], 2, 11)
         quantize(e_codes[1], e_scales[1], e_int[1], E4M3X4)
-        combine(acc[10], 10)
-        combine(acc[11], 11)
-        s_interleave(w_int[2], w_raw[2], 0, B)
-        quantize(e_codes[2], e_scales[2], e_int[2], E4M3X4)
-        h_acc = [bank(m) for m in range(4)]
-        for m in range(4):
-            mm2(h_acc[m], 0, m)
-        combine(acc[12], 12)
+        mm1(acc[11], 3, 11)
+        acc[13] = bank(5)
+        mm1(acc[13], 0, 13)
+        v_interleave(e_int[3], e_raw[3], 0, 128)
+        acc[14] = bank(6)
+        mm1(acc[14], 0, 14)
+        combine(acc[11], 11, (nc.sync, nc.sync, nc.sync, nc.sync))
+        mm1(acc[9], 3, 9)
+        s_interleave(e_int[2], e_raw[2], 0, 512)
+        mm1(acc[8], 3, 8)
+        combine(acc[9], 9, (nc.sync, nc.sync, nc.sync, nc.sync))
+        mm1(acc[10], 3, 10)
+        mm1(acc[13], 1, 13)
+        combine(acc[8], 8, (nc.sync, nc.sync, nc.sync, nc.sync))
+        mm1(acc[14], 1, 14)
+        acc[15] = bank(7)
+        mm1(acc[15], 0, 15)
+        combine(acc[10], 10, (nc.sync, nc.sync, nc.sync, nc.sync))
+        mm1(acc[15], 1, 15)
+        mm1(acc[13], 2, 13)
         quantize(w_codes[1], w_scales[1], w_int[1], E5M2X4)
-        for m in range(4):
-            mm2(h_acc[m], 1, m)
-        combine(acc[13], 13)
-        combine(acc[14], 14)
-        combine(acc[15], 15)
-        quantize(e_codes[3], e_scales[3], e_int[3], E4M3X4)
-        v_interleave(w_int[3], w_raw[3], 0, V_COLS)
-        s_interleave(w_int[3], w_raw[3], V_COLS, B)
+        acc[12] = bank(4)
+        mm1(acc[12], 0, 12)
+        mm1(acc[12], 1, 12)
+        s_interleave(w_int[2], w_raw[2], 128, 512)
+        v_interleave(w_int[2], w_raw[2], 0, 128)
+        mm1(acc[14], 2, 14)
+        mm1(acc[15], 2, 15)
+        quantize(e_codes[2], e_scales[2], e_int[2], E4M3X4)
+        mm1(acc[13], 3, 13)
+        mm1(acc[14], 3, 14)
+        combine(acc[13], 13, (nc.sync, nc.sync, nc.sync, nc.sync))
+        mm1(acc[15], 3, 15)
+        mm1(acc[12], 2, 12)
+        combine(acc[15], 15, (nc.sync, nc.sync, nc.sync, nc.sync))
+        mm1(acc[12], 3, 12)
+        s_interleave(e_int[3], e_raw[3], 128, 512)
+        h_acc[1] = bank(1)
+        mm2(h_acc[1], 0, 1)
+        combine(acc[12], 12, (nc.sync, nc.sync, nc.sync, nc.sync))
+        h_acc[0] = bank(0)
+        mm2(h_acc[0], 0, 0)
+        mm2(h_acc[1], 1, 1)
+        combine(acc[14], 14, (nc.sync, nc.sync, nc.sync, nc.sync))
+        h_acc[3] = bank(3)
+        mm2(h_acc[3], 0, 3)
+        mm2(h_acc[3], 1, 3)
         quantize(w_codes[2], w_scales[2], w_int[2], E5M2X4)
+        h_acc[2] = bank(2)
+        mm2(h_acc[2], 0, 2)
+        mm2(h_acc[2], 1, 2)
+        s_interleave(w_int[3], w_raw[3], 256, 512)
+        v_interleave(w_int[3], w_raw[3], 0, 256)
+        mm2(h_acc[1], 2, 1)
+        mm2(h_acc[3], 2, 3)
+        mm2(h_acc[2], 2, 2)
+        quantize(e_codes[3], e_scales[3], e_int[3], E4M3X4)
+        mm2(h_acc[0], 1, 0)
+        mm2(h_acc[0], 2, 0)
         quantize(w_codes[3], w_scales[3], w_int[3], E5M2X4)
-        for jg, m in ((2, 0), (2, 1), (3, 0), (2, 2), (3, 1), (2, 3), (3, 2), (3, 3)):
-            mm2(h_acc[m], jg, m)
-        for m in range(4):
-            res = sb([P, B], F32, "res%d" % m)
-            nc.vector.scalar_tensor_tensor(
-                out=res[:], in0=h_acc[m][:], scalar=coef[:, 16 + m : 17 + m], in1=rho_all[:], op0=MULT, op1=MULT,
-            )
-            nc.sync.dma_start(out=out[128 * m : 128 * (m + 1), :], in_=res[:])
+        mm2(h_acc[0], 3, 0)
+        mm2(h_acc[2], 3, 2)
+        finish(h_acc[0], 0)
+        mm2(h_acc[1], 3, 1)
+        mm2(h_acc[3], 3, 3)
+        finish(h_acc[2], 2)
+        finish(h_acc[3], 3)
+        finish(h_acc[1], 1)

@@ -98,11 +98,11 @@ def tile_scaled_block_projection_s9_kernel(tc, dirs, a_words, a_scales, pot, rho
 
         def load_rows():
             for g in range(len(FLAT), GROUPS):
-                nc.gpsimd.dma_start(
+                nc.sync.dma_start(
                     out=rows[4 * g : 4 * g + 4, :].rearrange("t (s r) -> t s r", r=4),
                     in_=pot[512 * g : 512 * (g + 1)].rearrange("(s t r) -> t s r", t=4, r=4),
                 )
-            nc.gpsimd.dma_start(out=rows[16:20, :], in_=rho.rearrange("(m x) -> m x", x=P))
+            nc.sync.dma_start(out=rows[16:20, :], in_=rho.rearrange("(m x) -> m x", x=P))
 
         def perm_scales(j):
             h, k = divmod(j, 2)
@@ -117,9 +117,9 @@ def tile_scaled_block_projection_s9_kernel(tc, dirs, a_words, a_scales, pot, rho
                 in_=a_raw[g][:, 1024 * j : 1024 * (j + 1)].bitcast(I32).rearrange("p (s t e) -> p t s e", t=4, e=2),
             )
 
+        nc.vector.memset(rows[:], 0.0)
         for h in range(2):
             nc.vector.memset(s_raw[h][:].rearrange("p g n -> p (g n)").bitcast(I32), 0)
-        nc.gpsimd.memset(rows[:], 0.0)
         make_identity(nc, ident[:])
 
         def v_interleave(dst, src, lo, hi):
@@ -184,197 +184,197 @@ def tile_scaled_block_projection_s9_kernel(tc, dirs, a_words, a_scales, pot, rho
         turned = bank(7, BF16, P)
         acc = [None] * 16
         h_acc = [None] * 4
-        load_d(0)
         load_a(0, 0, 1024)
-        load_scales(0)
-        load_a(1, 0, 1024)
-        load_d(1)
-        load_d(2)
-        v_interleave(d_int[0], d_raw[0], 0, 448)
-        s_interleave(d_int[0], d_raw[0], 448, 512)
-        load_d(3)
-        load_a(3, 0, 1024)
-        perm_words(0, 0)
         load_rows()
-        quantize(d_codes[0], d_scales[0], d_int[0], E4M3X4)
-        load_a(2, 0, 1024)
-        perm_scales(0)
+        load_d(0)
+        load_a(1, 0, 1024)
+        perm_words(0, 0)
+        load_scales(0)
+        nc.tensor.transpose(turned[:], rows[:], ident[:])
         perm_words(0, 1)
-        acc[0] = bank(0)
-        mm1(acc[0], 0, 0)
+        load_d(1)
+        nc.scalar.copy(out=coef[:], in_=turned[:, 0:20])
+        load_d(2)
+        load_d(3)
+        v_interleave(d_int[0], d_raw[0], 0, 320)
+        s_interleave(d_int[0], d_raw[0], 320, 512)
+        load_a(2, 0, 1024)
         perm_words(1, 0)
-        perm_scales(1)
-        acc[1] = bank(1)
-        mm1(acc[1], 0, 1)
+        load_a(3, 0, 1024)
         perm_words(1, 1)
-        acc[3] = bank(3)
-        mm1(acc[3], 0, 3)
-        v_interleave(d_int[1], d_raw[1], 0, 320)
-        s_interleave(d_int[1], d_raw[1], 320, 512)
+        quantize(d_codes[0], d_scales[0], d_int[0], E4M3X4)
+        perm_scales(0)
+        perm_scales(1)
         acc[2] = bank(2)
         mm1(acc[2], 0, 2)
-        acc[4] = bank(4)
-        mm1(acc[4], 0, 4)
         acc[6] = bank(6)
         mm1(acc[6], 0, 6)
-        quantize(d_codes[1], d_scales[1], d_int[1], E4M3X4)
         load_e(0)
-        s_interleave(d_int[2], d_raw[2], 320, 512)
-        v_interleave(d_int[2], d_raw[2], 0, 320)
-        mm1(acc[3], 1, 3)
-        mm1(acc[6], 1, 6)
-        load_a(0, 1024, 2048)
-        s_interleave(d_int[3], d_raw[3], 192, 512)
-        mm1(acc[1], 1, 1)
-        v_interleave(d_int[3], d_raw[3], 0, 192)
-        mm1(acc[2], 1, 2)
-        nc.tensor.transpose(turned[:], rows[:], ident[:])
-        quantize(d_codes[2], d_scales[2], d_int[2], E4M3X4)
+        v_interleave(d_int[1], d_raw[1], 0, 320)
+        s_interleave(d_int[1], d_raw[1], 320, 512)
         acc[5] = bank(5)
         mm1(acc[5], 0, 5)
-        mm1(acc[0], 1, 0)
-        perm_words(2, 0)
-        perm_words(3, 0)
-        nc.scalar.copy(out=coef[:], in_=turned[:, 0:20])
-        mm1(acc[1], 2, 1)
-        quantize(d_codes[3], d_scales[3], d_int[3], E4M3X4)
-        load_e(1)
-        mm1(acc[0], 2, 0)
-        nc.sync.dma_start(out=rho_all[:], in_=rho.partition_broadcast(P))
-        mm1(acc[2], 2, 2)
-        perm_words(2, 1)
+        acc[0] = bank(0)
+        mm1(acc[0], 0, 0)
+        quantize(d_codes[1], d_scales[1], d_int[1], E4M3X4)
+        acc[3] = bank(3)
+        mm1(acc[3], 0, 3)
         load_a(1, 1024, 2048)
+        s_interleave(d_int[2], d_raw[2], 320, 512)
+        acc[4] = bank(4)
+        mm1(acc[4], 0, 4)
+        v_interleave(d_int[2], d_raw[2], 0, 320)
+        mm1(acc[0], 1, 0)
+        mm1(acc[3], 1, 3)
+        s_interleave(d_int[3], d_raw[3], 192, 512)
+        v_interleave(d_int[3], d_raw[3], 0, 192)
+        mm1(acc[2], 1, 2)
+        acc[1] = bank(1)
+        mm1(acc[1], 0, 1)
+        perm_words(2, 0)
+        mm1(acc[1], 1, 1)
+        quantize(d_codes[2], d_scales[2], d_int[2], E4M3X4)
+        mm1(acc[5], 1, 5)
+        mm1(acc[4], 1, 4)
+        perm_words(3, 0)
+        mm1(acc[0], 2, 0)
+        load_e(1)
+        quantize(d_codes[3], d_scales[3], d_int[3], E4M3X4)
+        mm1(acc[2], 2, 2)
+        mm1(acc[1], 2, 1)
+        perm_words(2, 1)
         mm1(acc[2], 3, 2)
         perm_words(3, 1)
         s_interleave(e_int[0], e_raw[0], 64, 512)
-        mm1(acc[6], 2, 6)
+        mm1(acc[4], 2, 4)
         v_interleave(e_int[0], e_raw[0], 0, 64)
         combine(acc[2], 2, (nc.sync, nc.sync, nc.sync, nc.sync))
         mm1(acc[3], 2, 3)
+        load_scales(1)
+        mm1(acc[3], 3, 3)
+        perm_words(1, 3)
+        mm1(acc[0], 3, 0)
+        combine(acc[3], 3, (nc.sync, nc.sync, nc.sync, nc.sync))
+        load_a(0, 1024, 2048)
+        mm1(acc[1], 3, 1)
+        load_a(2, 1024, 2048)
         acc[7] = bank(7)
         mm1(acc[7], 0, 7)
-        perm_words(0, 2)
-        mm1(acc[1], 3, 1)
-        perm_words(0, 3)
-        mm1(acc[3], 3, 3)
         combine(acc[1], 1, (nc.sync, nc.sync, nc.sync, nc.sync))
-        mm1(acc[0], 3, 0)
-        load_scales(1)
-        mm1(acc[4], 1, 4)
-        load_a(2, 1024, 2048)
-        combine(acc[0], 0, (nc.sync, nc.sync, nc.sync, nc.sync))
-        mm1(acc[5], 1, 5)
-        load_a(3, 1024, 2048)
-        s_interleave(e_int[1], e_raw[1], 0, 512)
         mm1(acc[7], 1, 7)
-        combine(acc[3], 3, (nc.sync, nc.sync, nc.sync, nc.sync))
-        mm1(acc[5], 2, 5)
         mm1(acc[7], 2, 7)
-        quantize(e_codes[0], e_scales[0], e_int[0], E4M3X4)
-        mm1(acc[7], 3, 7)
-        mm1(acc[5], 3, 5)
+        s_interleave(e_int[1], e_raw[1], 0, 512)
         perm_words(1, 2)
-        mm1(acc[4], 2, 4)
-        combine(acc[7], 7, (nc.sync, nc.sync, nc.sync, nc.sync))
-        load_e(2)
         mm1(acc[4], 3, 4)
-        mm1(acc[6], 3, 6)
-        combine(acc[5], 5, (nc.sync, nc.sync, nc.sync, nc.sync))
-        s_interleave(w_int[0], w_raw[0], 0, 512)
-        perm_scales(2)
+        combine(acc[0], 0, (nc.sync, nc.sync, nc.sync, nc.sync))
+        mm1(acc[7], 3, 7)
+        mm1(acc[5], 2, 5)
+        load_e(2)
         combine(acc[4], 4, (nc.sync, nc.sync, nc.sync, nc.sync))
+        mm1(acc[5], 3, 5)
+        load_a(3, 1024, 2048)
+        mm1(acc[6], 1, 6)
+        combine(acc[5], 5, (nc.sync, nc.sync, nc.sync, nc.sync))
+        mm1(acc[6], 2, 6)
+        mm1(acc[6], 3, 6)
+        perm_scales(2)
+        perm_words(0, 2)
+        s_interleave(w_int[0], w_raw[0], 0, 512)
+        perm_words(0, 3)
         acc[9] = bank(1)
         mm1(acc[9], 0, 9)
-        load_e(3)
+        perm_words(2, 2)
         acc[8] = bank(0)
         mm1(acc[8], 0, 8)
         combine(acc[6], 6, (nc.sync, nc.sync, nc.sync, nc.sync))
+        load_e(3)
+        mm1(acc[9], 1, 9)
         acc[10] = bank(2)
         mm1(acc[10], 0, 10)
-        acc[11] = bank(3)
-        mm1(acc[11], 0, 11)
-        perm_words(2, 2)
-        mm1(acc[9], 1, 9)
         perm_scales(3)
         mm1(acc[8], 1, 8)
-        perm_words(2, 3)
-        mm1(acc[10], 1, 10)
-        s_interleave(w_int[1], w_raw[1], 0, 512)
-        perm_words(3, 2)
-        mm1(acc[11], 1, 11)
-        perm_words(1, 3)
-        mm1(acc[9], 2, 9)
-        perm_words(3, 3)
-        quantize(w_codes[0], w_scales[0], w_int[0], E5M2X4)
-        mm1(acc[8], 2, 8)
-        mm1(acc[10], 2, 10)
-        mm1(acc[11], 2, 11)
-        quantize(e_codes[1], e_scales[1], e_int[1], E4M3X4)
-        mm1(acc[11], 3, 11)
+        combine(acc[7], 7, (nc.sync, nc.sync, nc.sync, nc.sync))
         acc[13] = bank(5)
         mm1(acc[13], 0, 13)
-        v_interleave(e_int[3], e_raw[3], 0, 128)
         acc[14] = bank(6)
         mm1(acc[14], 0, 14)
-        combine(acc[11], 11, (nc.sync, nc.sync, nc.sync, nc.sync))
-        mm1(acc[9], 3, 9)
-        s_interleave(e_int[2], e_raw[2], 0, 512)
-        mm1(acc[8], 3, 8)
-        combine(acc[9], 9, (nc.sync, nc.sync, nc.sync, nc.sync))
-        mm1(acc[10], 3, 10)
-        mm1(acc[13], 1, 13)
-        combine(acc[8], 8, (nc.sync, nc.sync, nc.sync, nc.sync))
+        perm_words(2, 3)
         mm1(acc[14], 1, 14)
-        acc[15] = bank(7)
-        mm1(acc[15], 0, 15)
-        combine(acc[10], 10, (nc.sync, nc.sync, nc.sync, nc.sync))
-        mm1(acc[15], 1, 15)
-        mm1(acc[13], 2, 13)
-        quantize(w_codes[1], w_scales[1], w_int[1], E5M2X4)
+        perm_words(3, 2)
         acc[12] = bank(4)
         mm1(acc[12], 0, 12)
+        perm_words(3, 3)
+        s_interleave(w_int[1], w_raw[1], 0, 512)
+        quantize(e_codes[1], e_scales[1], e_int[1], E4M3X4)
+        mm1(acc[9], 2, 9)
+        nc.sync.dma_start(out=rho_all[:], in_=rho.partition_broadcast(P))
+        mm1(acc[9], 3, 9)
+        mm1(acc[8], 2, 8)
+        quantize(w_codes[0], w_scales[0], w_int[0], E5M2X4)
+        mm1(acc[10], 1, 10)
+        mm1(acc[10], 2, 10)
+        combine(acc[9], 9, (nc.sync, nc.sync, nc.sync, nc.sync))
+        mm1(acc[10], 3, 10)
+        acc[11] = bank(3)
+        mm1(acc[11], 0, 11)
+        quantize(e_codes[0], e_scales[0], e_int[0], E4M3X4)
+        mm1(acc[11], 1, 11)
+        mm1(acc[11], 2, 11)
+        combine(acc[10], 10, (nc.sync, nc.sync, nc.sync, nc.sync))
+        s_interleave(e_int[2], e_raw[2], 0, 512)
+        mm1(acc[8], 3, 8)
+        mm1(acc[11], 3, 11)
+        combine(acc[8], 8, (nc.sync, nc.sync, nc.sync, nc.sync))
+        acc[15] = bank(7)
+        mm1(acc[15], 0, 15)
         mm1(acc[12], 1, 12)
-        s_interleave(w_int[2], w_raw[2], 128, 512)
+        combine(acc[11], 11, (nc.sync, nc.sync, nc.sync, nc.sync))
+        mm1(acc[13], 1, 13)
+        mm1(acc[13], 2, 13)
+        v_interleave(e_int[3], e_raw[3], 0, 128)
+        mm1(acc[15], 1, 15)
         v_interleave(w_int[2], w_raw[2], 0, 128)
-        mm1(acc[14], 2, 14)
         mm1(acc[15], 2, 15)
-        quantize(e_codes[2], e_scales[2], e_int[2], E4M3X4)
-        mm1(acc[13], 3, 13)
-        mm1(acc[14], 3, 14)
-        combine(acc[13], 13, (nc.sync, nc.sync, nc.sync, nc.sync))
-        mm1(acc[15], 3, 15)
-        mm1(acc[12], 2, 12)
-        combine(acc[15], 15, (nc.sync, nc.sync, nc.sync, nc.sync))
-        mm1(acc[12], 3, 12)
-        s_interleave(e_int[3], e_raw[3], 128, 512)
+        mm1(acc[14], 2, 14)
+        quantize(w_codes[1], w_scales[1], w_int[1], E5M2X4)
+        s_interleave(w_int[2], w_raw[2], 128, 512)
         h_acc[1] = bank(1)
         mm2(h_acc[1], 0, 1)
-        combine(acc[12], 12, (nc.sync, nc.sync, nc.sync, nc.sync))
-        h_acc[0] = bank(0)
-        mm2(h_acc[0], 0, 0)
-        mm2(h_acc[1], 1, 1)
+        mm1(acc[13], 3, 13)
+        quantize(e_codes[2], e_scales[2], e_int[2], E4M3X4)
+        mm1(acc[15], 3, 15)
+        mm1(acc[14], 3, 14)
+        combine(acc[15], 15, (nc.sync, nc.sync, nc.sync, nc.sync))
+        mm1(acc[12], 2, 12)
+        mm1(acc[12], 3, 12)
         combine(acc[14], 14, (nc.sync, nc.sync, nc.sync, nc.sync))
-        h_acc[3] = bank(3)
-        mm2(h_acc[3], 0, 3)
-        mm2(h_acc[3], 1, 3)
-        quantize(w_codes[2], w_scales[2], w_int[2], E5M2X4)
         h_acc[2] = bank(2)
         mm2(h_acc[2], 0, 2)
+        s_interleave(e_int[3], e_raw[3], 128, 512)
+        h_acc[0] = bank(0)
+        mm2(h_acc[0], 0, 0)
+        combine(acc[12], 12, (nc.sync, nc.sync, nc.sync, nc.sync))
+        h_acc[3] = bank(3)
+        mm2(h_acc[3], 0, 3)
         mm2(h_acc[2], 1, 2)
+        combine(acc[13], 13, (nc.sync, nc.sync, nc.sync, nc.sync))
+        mm2(h_acc[3], 1, 3)
+        mm2(h_acc[1], 1, 1)
+        quantize(w_codes[2], w_scales[2], w_int[2], E5M2X4)
+        mm2(h_acc[0], 1, 0)
         s_interleave(w_int[3], w_raw[3], 256, 512)
         v_interleave(w_int[3], w_raw[3], 0, 256)
+        mm2(h_acc[2], 2, 2)
         mm2(h_acc[1], 2, 1)
         mm2(h_acc[3], 2, 3)
-        mm2(h_acc[2], 2, 2)
         quantize(e_codes[3], e_scales[3], e_int[3], E4M3X4)
-        mm2(h_acc[0], 1, 0)
         mm2(h_acc[0], 2, 0)
         quantize(w_codes[3], w_scales[3], w_int[3], E5M2X4)
-        mm2(h_acc[0], 3, 0)
-        mm2(h_acc[2], 3, 2)
-        finish(h_acc[0], 0)
         mm2(h_acc[1], 3, 1)
+        mm2(h_acc[2], 3, 2)
+        finish(h_acc[1], 1)
+        mm2(h_acc[0], 3, 0)
         mm2(h_acc[3], 3, 3)
         finish(h_acc[2], 2)
         finish(h_acc[3], 3)
-        finish(h_acc[1], 1)
+        finish(h_acc[0], 0)

@@ -43,27 +43,26 @@ def tile_scaled_block_projection_s9_kernel(tc, dirs, a_words, a_scales, pot, rho
             return psum.tile([P, cols], dtype, name="bank%d" % i, tag="bank%d" % i)
 
         G = range(GROUPS)
+        REGROUPED = (1, 2)
+        MOVED = (0, 3)
         d_raw = [sb([P, 4, B], BF16, "d_raw%d" % g) for g in G]
         d_int = [sb([P, B, 4], BF16, "d_int%d" % g) for g in G]
         d_codes = [sb([P, B], U32, "d_codes%d" % g) for g in G]
         d_scales = [sb([P, B], U8, "d_scales%d" % g) for g in G]
-        FLAT = ()
-        e_raw = [sb([P, 4, B], BF16, "e_raw%d" % g) for g in G]
-        e_int = [None if g in FLAT else sb([P, B, 4], BF16, "e_int%d" % g) for g in G]
-        e_codes = [d_codes[g] if g in FLAT else sb([P, B], U32, "e_codes%d" % g) for g in G]
-        e_scales = [d_scales[g] if g in FLAT else sb([P, B], U8, "e_scales%d" % g) for g in G]
-        a_perm = [[None if j in FLAT else sb([P, 1024], U8, "a_perm%d_%d" % (g, j)) for j in G] for g in G]
-        s_perm = [None if j in FLAT else sb([P, GROUPS, B], U8, "s_perm%d" % j) for j in G]
-        w_flat = [sb([P, B], BF16, "w_flat%d" % i) for i in range(4 * len(FLAT))]
+        d_flat = {g: sb([P, 4, B], BF16, "d_flat%d" % g) for g in REGROUPED}
+        w_flat = {g: sb([P, 4, B], BF16, "w_flat%d" % g) for g in REGROUPED}
         w_raw = [sb([P, 4, B], BF16, "w_raw%d" % g) for g in G]
         w_int = [sb([P, B, 4], BF16, "w_int%d" % g) for g in G]
         w_codes = [sb([P, B], U32, "w_codes%d" % g) for g in G]
         w_scales = [sb([P, B], U8, "w_scales%d" % g) for g in G]
         a_raw = [sb([P, 2 * K], U8, "a_raw%d" % g) for g in G]
         s_raw = [sb([P, GROUPS, K // 2], U8, "s_raw%d" % h) for h in range(2)]
+        a_moved = {(g, j): sb([P, 1024], U8, "a_moved%d_%d" % (g, j)) for g in G for j in MOVED}
+        s_moved = {j: sb([P, GROUPS, B], U8, "s_moved%d" % j) for j in MOVED}
+        pot_moved = {j: sb([P, 4], BF16, "pot_moved%d" % j) for j in MOVED}
         rows = sb([P, P], BF16, "rows")
         ident = sb([P, P], BF16, "ident")
-        coef = sb([P, 20], F32, "coef")
+        coef = sb([P, 12], F32, "coef")
         rho_all = sb([P, B], BF16, "rho_all")
 
         def load_scales(h):
@@ -88,34 +87,18 @@ def tile_scaled_block_projection_s9_kernel(tc, dirs, a_words, a_scales, pot, rho
             )
 
         def load_e(g):
-            src = dirs[512 * g : 512 * (g + 1), :]
-            if g in FLAT:
-                nc.sync.dma_start(out=e_raw[g][:], in_=src.rearrange("(m p) b -> p m b", m=4))
-            else:
-                quads = src.rearrange("(s t r) b -> r s t b", t=4, r=4)
-                for r in range(4):
-                    nc.sync.dma_start(out=e_raw[g][r : 128 : 4, :, :], in_=quads[r])
+            nc.sync.dma_start(
+                out=d_flat[g][:],
+                in_=dirs[512 * g : 512 * (g + 1), :].rearrange("(m p) b -> p m b", m=4),
+            )
 
         def load_rows():
-            for g in range(len(FLAT), GROUPS):
-                nc.sync.dma_start(
-                    out=rows[4 * g : 4 * g + 4, :].rearrange("t (s r) -> t s r", r=4),
-                    in_=pot[512 * g : 512 * (g + 1)].rearrange("(s t r) -> t s r", t=4, r=4),
-                )
-            nc.sync.dma_start(out=rows[16:20, :], in_=rho.rearrange("(m x) -> m x", x=P))
-
-        def perm_scales(j):
-            h, k = divmod(j, 2)
-            nc.vector.tensor_copy(
-                out=s_perm[j][:].bitcast(I32).rearrange("p g (t s) -> p g t s", t=4),
-                in_=s_raw[h][:, :, 512 * k : 512 * (k + 1)].bitcast(I32).rearrange("p g (s t) -> p g t s", t=4),
+            for j in MOVED:
+                nc.sync.dma_start(out=pot_moved[j][:], in_=pot[512 * j : 512 * (j + 1)].rearrange("(p t) -> p t", t=4))
+            nc.sync.dma_start(
+                out=rows[0:8, :], in_=pot[512 : 1536].rearrange("(i x) -> i x", x=P)
             )
-
-        def perm_words(g, j):
-            nc.vector.tensor_copy(
-                out=a_perm[g][j][:].bitcast(I32).rearrange("p (t s e) -> p t s e", t=4, e=2),
-                in_=a_raw[g][:, 1024 * j : 1024 * (j + 1)].bitcast(I32).rearrange("p (s t e) -> p t s e", t=4, e=2),
-            )
+            nc.sync.dma_start(out=rows[8:12, :], in_=rho.rearrange("(m x) -> m x", x=P))
 
         nc.vector.memset(rows[:], 0.0)
         for h in range(2):
@@ -133,15 +116,27 @@ def tile_scaled_block_projection_s9_kernel(tc, dirs, a_words, a_scales, pot, rho
                 out=codes[:].bitcast(fmt), scales=scales[:], in_=src[:].rearrange("p b t -> p (b t)")
             )
 
+        def move_scales(j):
+            h, k = divmod(j, 2)
+            nc.vector.tensor_copy(
+                out=s_moved[j][:].rearrange("p g (t m) -> p g t m", t=4),
+                in_=s_raw[h][:, :, 512 * k : 512 * (k + 1)].rearrange("p g (m t) -> p g t m", t=4),
+            )
+
+        def move_words(g, j):
+            nc.vector.tensor_copy(
+                out=a_moved[g, j][:].rearrange("p (t m e) -> p t m e", t=4, e=2),
+                in_=a_raw[g][:, 1024 * j : 1024 * (j + 1)].rearrange("p (m t e) -> p t m e", t=4, e=2),
+            )
+
         def mm1(acc, g, i):
             j, n = divmod(i, 4)
-            if j in FLAT:
-                h = i // 8
-                words = a_raw[g][:, 256 * i : 256 * (i + 1)]
-                scales = s_raw[h][:, g, 128 * (i % 8) : 128 * (i % 8 + 1)]
+            if j in MOVED:
+                words = a_moved[g, j][:, 256 * n : 256 * (n + 1)]
+                scales = s_moved[j][:, g, 128 * n : 128 * (n + 1)]
             else:
-                words = a_perm[g][j][:, 256 * n : 256 * (n + 1)]
-                scales = s_perm[j][:, g, 128 * n : 128 * (n + 1)]
+                words = a_raw[g][:, 256 * i : 256 * (i + 1)]
+                scales = s_raw[i // 8][:, g, 128 * (i % 8) : 128 * (i % 8 + 1)]
             nc.tensor.matmul_mx(
                 out=acc[:],
                 lhsT=words.bitcast(E2M1X4),
@@ -152,22 +147,27 @@ def tile_scaled_block_projection_s9_kernel(tc, dirs, a_words, a_scales, pot, rho
                 stop=(g == GROUPS - 1),
             )
 
-        def combine(acc, i, queues):
+        def combine(acc, i):
             j, n = divmod(i, 4)
+            if j in MOVED:
+                w, d, v = w_raw[j], d_raw[j], pot_moved[j][:, n : n + 1]
+            else:
+                w, d, v = w_flat[j], d_flat[j], coef[:, i - 4 : i - 3]
             nc.vector.scalar_tensor_tensor(
-                out=w_flat[i][:] if j in FLAT else w_raw[j][:, n, :], in0=e_raw[j][:, n, :], scalar=coef[:, i : i + 1],
-                in1=acc[:], op0=MULT, op1=ADD,
+                out=w[:, n, :], in0=d[:, n, :], scalar=v, in1=acc[:], op0=MULT, op1=ADD
             )
-            if j in FLAT:
-                for t in range(4):
-                    queues[t].dma_start(out=w_raw[j][32 * n : 32 * n + 32, t, :], in_=w_flat[i][t : 128 : 4, :])
+
+        def regroup(i):
+            j, n = divmod(i, 4)
+            for t in range(4):
+                nc.sync.dma_start(out=w_raw[j][32 * n : 32 * n + 32, t, :], in_=w_flat[j][t : 128 : 4, n, :])
 
         def mm2(acc, j, m):
             cols = slice(128 * m, 128 * (m + 1))
             nc.tensor.matmul_mx(
                 out=acc[:],
-                lhsT=e_codes[j][:, cols].bitcast(E4M3X4),
-                lhsT_scale=e_scales[j][:, cols],
+                lhsT=d_codes[j][:, cols].bitcast(E4M3X4),
+                lhsT_scale=d_scales[j][:, cols],
                 rhs=w_codes[j][:].bitcast(E5M2X4),
                 rhs_scale=w_scales[j][:],
                 start=(j == 0),
@@ -177,204 +177,189 @@ def tile_scaled_block_projection_s9_kernel(tc, dirs, a_words, a_scales, pot, rho
         def finish(acc_m, m):
             res = sb([P, B], F32, "res%d" % m)
             nc.vector.scalar_tensor_tensor(
-                out=res[:], in0=acc_m[:], scalar=coef[:, 16 + m : 17 + m], in1=rho_all[:], op0=MULT, op1=MULT,
+                out=res[:], in0=acc_m[:], scalar=coef[:, 8 + m : 9 + m], in1=rho_all[:], op0=MULT, op1=MULT,
             )
             nc.sync.dma_start(out=out[128 * m : 128 * (m + 1), :], in_=res[:])
 
         turned = bank(7, BF16, P)
         acc = [None] * 16
         h_acc = [None] * 4
+        load_d(0)
+        load_scales(0)
         load_a(0, 0, 1024)
         load_rows()
-        load_d(0)
-        load_a(1, 0, 1024)
-        perm_words(0, 0)
-        load_scales(0)
-        nc.tensor.transpose(turned[:], rows[:], ident[:])
-        perm_words(0, 1)
         load_d(1)
-        nc.scalar.copy(out=coef[:], in_=turned[:, 0:20])
+        s_interleave(d_int[0], d_raw[0], 0, 512)
         load_d(2)
         load_d(3)
-        v_interleave(d_int[0], d_raw[0], 0, 320)
-        s_interleave(d_int[0], d_raw[0], 320, 512)
+        load_a(1, 0, 1024)
         load_a(2, 0, 1024)
-        perm_words(1, 0)
+        move_scales(0)
+        load_a(3, 1024, 2048)
+        nc.tensor.transpose(turned[:], rows[:], ident[:])
+        load_a(0, 1024, 2048)
         load_a(3, 0, 1024)
-        perm_words(1, 1)
+        move_words(0, 0)
+        nc.scalar.copy(out=coef[:], in_=turned[:, 0:12])
         quantize(d_codes[0], d_scales[0], d_int[0], E4M3X4)
-        perm_scales(0)
-        perm_scales(1)
-        acc[2] = bank(2)
-        mm1(acc[2], 0, 2)
-        acc[6] = bank(6)
-        mm1(acc[6], 0, 6)
-        load_e(0)
-        v_interleave(d_int[1], d_raw[1], 0, 320)
-        s_interleave(d_int[1], d_raw[1], 320, 512)
-        acc[5] = bank(5)
-        mm1(acc[5], 0, 5)
-        acc[0] = bank(0)
-        mm1(acc[0], 0, 0)
-        quantize(d_codes[1], d_scales[1], d_int[1], E4M3X4)
-        acc[3] = bank(3)
-        mm1(acc[3], 0, 3)
-        load_a(1, 1024, 2048)
-        s_interleave(d_int[2], d_raw[2], 320, 512)
-        acc[4] = bank(4)
-        mm1(acc[4], 0, 4)
-        v_interleave(d_int[2], d_raw[2], 0, 320)
-        mm1(acc[0], 1, 0)
-        mm1(acc[3], 1, 3)
-        s_interleave(d_int[3], d_raw[3], 192, 512)
-        v_interleave(d_int[3], d_raw[3], 0, 192)
-        mm1(acc[2], 1, 2)
+        load_e(1)
+        s_interleave(d_int[1], d_raw[1], 192, 512)
+        v_interleave(d_int[1], d_raw[1], 0, 192)
         acc[1] = bank(1)
         mm1(acc[1], 0, 1)
-        perm_words(2, 0)
-        mm1(acc[1], 1, 1)
-        quantize(d_codes[2], d_scales[2], d_int[2], E4M3X4)
-        mm1(acc[5], 1, 5)
-        mm1(acc[4], 1, 4)
-        perm_words(3, 0)
-        mm1(acc[0], 2, 0)
-        load_e(1)
-        quantize(d_codes[3], d_scales[3], d_int[3], E4M3X4)
-        mm1(acc[2], 2, 2)
-        mm1(acc[1], 2, 1)
-        perm_words(2, 1)
-        mm1(acc[2], 3, 2)
-        perm_words(3, 1)
-        s_interleave(e_int[0], e_raw[0], 64, 512)
-        mm1(acc[4], 2, 4)
-        v_interleave(e_int[0], e_raw[0], 0, 64)
-        combine(acc[2], 2, (nc.sync, nc.sync, nc.sync, nc.sync))
-        mm1(acc[3], 2, 3)
+        acc[3] = bank(3)
+        mm1(acc[3], 0, 3)
         load_scales(1)
-        mm1(acc[3], 3, 3)
-        perm_words(1, 3)
-        mm1(acc[0], 3, 0)
-        combine(acc[3], 3, (nc.sync, nc.sync, nc.sync, nc.sync))
-        load_a(0, 1024, 2048)
-        mm1(acc[1], 3, 1)
-        load_a(2, 1024, 2048)
+        v_interleave(d_int[2], d_raw[2], 0, 256)
+        acc[0] = bank(0)
+        mm1(acc[0], 0, 0)
+        s_interleave(d_int[2], d_raw[2], 256, 512)
+        acc[4] = bank(4)
+        mm1(acc[4], 0, 4)
+        quantize(d_codes[1], d_scales[1], d_int[1], E4M3X4)
+        acc[2] = bank(2)
+        mm1(acc[2], 0, 2)
+        v_interleave(d_int[3], d_raw[3], 0, 64)
+        acc[6] = bank(6)
+        mm1(acc[6], 0, 6)
+        s_interleave(d_int[3], d_raw[3], 64, 512)
+        quantize(d_codes[2], d_scales[2], d_int[2], E4M3X4)
         acc[7] = bank(7)
         mm1(acc[7], 0, 7)
-        combine(acc[1], 1, (nc.sync, nc.sync, nc.sync, nc.sync))
         mm1(acc[7], 1, 7)
+        move_words(1, 0)
+        mm1(acc[4], 1, 4)
         mm1(acc[7], 2, 7)
-        s_interleave(e_int[1], e_raw[1], 0, 512)
-        perm_words(1, 2)
-        mm1(acc[4], 3, 4)
-        combine(acc[0], 0, (nc.sync, nc.sync, nc.sync, nc.sync))
-        mm1(acc[7], 3, 7)
-        mm1(acc[5], 2, 5)
+        mm1(acc[4], 2, 4)
+        move_words(2, 0)
+        mm1(acc[2], 1, 2)
         load_e(2)
-        combine(acc[4], 4, (nc.sync, nc.sync, nc.sync, nc.sync))
-        mm1(acc[5], 3, 5)
-        load_a(3, 1024, 2048)
-        mm1(acc[6], 1, 6)
-        combine(acc[5], 5, (nc.sync, nc.sync, nc.sync, nc.sync))
-        mm1(acc[6], 2, 6)
-        mm1(acc[6], 3, 6)
-        perm_scales(2)
-        perm_words(0, 2)
-        s_interleave(w_int[0], w_raw[0], 0, 512)
-        perm_words(0, 3)
-        acc[9] = bank(1)
-        mm1(acc[9], 0, 9)
-        perm_words(2, 2)
-        acc[8] = bank(0)
-        mm1(acc[8], 0, 8)
-        combine(acc[6], 6, (nc.sync, nc.sync, nc.sync, nc.sync))
-        load_e(3)
-        mm1(acc[9], 1, 9)
-        acc[10] = bank(2)
-        mm1(acc[10], 0, 10)
-        perm_scales(3)
-        mm1(acc[8], 1, 8)
-        combine(acc[7], 7, (nc.sync, nc.sync, nc.sync, nc.sync))
-        acc[13] = bank(5)
-        mm1(acc[13], 0, 13)
-        acc[14] = bank(6)
-        mm1(acc[14], 0, 14)
-        perm_words(2, 3)
-        mm1(acc[14], 1, 14)
-        perm_words(3, 2)
-        acc[12] = bank(4)
-        mm1(acc[12], 0, 12)
-        perm_words(3, 3)
-        s_interleave(w_int[1], w_raw[1], 0, 512)
-        quantize(e_codes[1], e_scales[1], e_int[1], E4M3X4)
-        mm1(acc[9], 2, 9)
+        mm1(acc[3], 1, 3)
+        move_words(3, 3)
+        mm1(acc[3], 2, 3)
+        load_a(2, 1024, 2048)
+        mm1(acc[0], 1, 0)
+        quantize(d_codes[3], d_scales[3], d_int[3], E4M3X4)
+        mm1(acc[0], 2, 0)
+        mm1(acc[2], 2, 2)
+        load_a(1, 1024, 2048)
+        mm1(acc[1], 1, 1)
+        move_words(3, 0)
+        mm1(acc[7], 3, 7)
+        mm1(acc[1], 2, 1)
+        move_words(0, 3)
+        mm1(acc[2], 3, 2)
+        mm1(acc[0], 3, 0)
+        combine(acc[2], 2)
+        mm1(acc[3], 3, 3)
         nc.sync.dma_start(out=rho_all[:], in_=rho.partition_broadcast(P))
-        mm1(acc[9], 3, 9)
-        mm1(acc[8], 2, 8)
-        quantize(w_codes[0], w_scales[0], w_int[0], E5M2X4)
-        mm1(acc[10], 1, 10)
-        mm1(acc[10], 2, 10)
-        combine(acc[9], 9, (nc.sync, nc.sync, nc.sync, nc.sync))
-        mm1(acc[10], 3, 10)
+        mm1(acc[1], 3, 1)
+        mm1(acc[4], 3, 4)
+        combine(acc[3], 3)
+        acc[5] = bank(5)
+        mm1(acc[5], 0, 5)
+        mm1(acc[5], 1, 5)
+        combine(acc[0], 0)
+        mm1(acc[5], 2, 5)
+        mm1(acc[5], 3, 5)
+        combine(acc[1], 1)
         acc[11] = bank(3)
         mm1(acc[11], 0, 11)
-        quantize(e_codes[0], e_scales[0], e_int[0], E4M3X4)
+        acc[10] = bank(2)
+        mm1(acc[10], 0, 10)
+        combine(acc[7], 7)
+        acc[9] = bank(1)
+        mm1(acc[9], 0, 9)
+        s_interleave(w_int[0], w_raw[0], 0, 512)
+        acc[8] = bank(0)
+        mm1(acc[8], 0, 8)
+        combine(acc[5], 5)
+        mm1(acc[6], 1, 6)
+        regroup(7)
+        mm1(acc[6], 2, 6)
+        mm1(acc[6], 3, 6)
+        combine(acc[4], 4)
+        regroup(5)
+        combine(acc[6], 6)
+        mm1(acc[10], 1, 10)
+        mm1(acc[8], 1, 8)
+        move_words(1, 3)
         mm1(acc[11], 1, 11)
+        regroup(4)
         mm1(acc[11], 2, 11)
-        combine(acc[10], 10, (nc.sync, nc.sync, nc.sync, nc.sync))
-        s_interleave(e_int[2], e_raw[2], 0, 512)
-        mm1(acc[8], 3, 8)
+        move_scales(3)
         mm1(acc[11], 3, 11)
-        combine(acc[8], 8, (nc.sync, nc.sync, nc.sync, nc.sync))
+        regroup(6)
+        mm1(acc[10], 2, 10)
+        mm1(acc[10], 3, 10)
+        mm1(acc[8], 2, 8)
+        mm1(acc[8], 3, 8)
+        combine(acc[11], 11)
+        acc[14] = bank(6)
+        mm1(acc[14], 0, 14)
+        mm1(acc[14], 1, 14)
+        combine(acc[8], 8)
+        regroup(11)
+        acc[12] = bank(4)
+        mm1(acc[12], 0, 12)
+        mm1(acc[12], 1, 12)
+        combine(acc[10], 10)
+        mm1(acc[9], 1, 9)
+        regroup(8)
+        mm1(acc[9], 2, 9)
+        move_words(2, 3)
+        mm1(acc[9], 3, 9)
+        s_interleave(w_int[1], w_raw[1], 0, 512)
+        acc[13] = bank(5)
+        mm1(acc[13], 0, 13)
+        mm1(acc[13], 1, 13)
+        combine(acc[9], 9)
+        regroup(10)
+        mm1(acc[14], 2, 14)
+        mm1(acc[14], 3, 14)
+        quantize(w_codes[0], w_scales[0], w_int[0], E5M2X4)
+        regroup(9)
+        mm1(acc[13], 2, 13)
+        mm1(acc[13], 3, 13)
+        combine(acc[14], 14)
+        mm1(acc[12], 2, 12)
+        mm1(acc[12], 3, 12)
+        combine(acc[13], 13)
         acc[15] = bank(7)
         mm1(acc[15], 0, 15)
-        mm1(acc[12], 1, 12)
-        combine(acc[11], 11, (nc.sync, nc.sync, nc.sync, nc.sync))
-        mm1(acc[13], 1, 13)
-        mm1(acc[13], 2, 13)
-        v_interleave(e_int[3], e_raw[3], 0, 128)
         mm1(acc[15], 1, 15)
-        v_interleave(w_int[2], w_raw[2], 0, 128)
         mm1(acc[15], 2, 15)
-        mm1(acc[14], 2, 14)
-        quantize(w_codes[1], w_scales[1], w_int[1], E5M2X4)
+        combine(acc[12], 12)
+        mm1(acc[15], 3, 15)
+        h_acc[0] = bank(0)
+        mm2(h_acc[0], 0, 0)
+        combine(acc[15], 15)
+        h_acc[2] = bank(2)
+        mm2(h_acc[2], 0, 2)
         s_interleave(w_int[2], w_raw[2], 128, 512)
         h_acc[1] = bank(1)
         mm2(h_acc[1], 0, 1)
-        mm1(acc[13], 3, 13)
-        quantize(e_codes[2], e_scales[2], e_int[2], E4M3X4)
-        mm1(acc[15], 3, 15)
-        mm1(acc[14], 3, 14)
-        combine(acc[15], 15, (nc.sync, nc.sync, nc.sync, nc.sync))
-        mm1(acc[12], 2, 12)
-        mm1(acc[12], 3, 12)
-        combine(acc[14], 14, (nc.sync, nc.sync, nc.sync, nc.sync))
-        h_acc[2] = bank(2)
-        mm2(h_acc[2], 0, 2)
-        s_interleave(e_int[3], e_raw[3], 128, 512)
-        h_acc[0] = bank(0)
-        mm2(h_acc[0], 0, 0)
-        combine(acc[12], 12, (nc.sync, nc.sync, nc.sync, nc.sync))
+        v_interleave(w_int[2], w_raw[2], 0, 128)
         h_acc[3] = bank(3)
         mm2(h_acc[3], 0, 3)
-        mm2(h_acc[2], 1, 2)
-        combine(acc[13], 13, (nc.sync, nc.sync, nc.sync, nc.sync))
-        mm2(h_acc[3], 1, 3)
-        mm2(h_acc[1], 1, 1)
+        v_interleave(w_int[3], w_raw[3], 0, 320)
+        quantize(w_codes[1], w_scales[1], w_int[1], E5M2X4)
+        s_interleave(w_int[3], w_raw[3], 320, 512)
         quantize(w_codes[2], w_scales[2], w_int[2], E5M2X4)
-        mm2(h_acc[0], 1, 0)
-        s_interleave(w_int[3], w_raw[3], 256, 512)
-        v_interleave(w_int[3], w_raw[3], 0, 256)
-        mm2(h_acc[2], 2, 2)
+        mm2(h_acc[1], 1, 1)
+        mm2(h_acc[3], 1, 3)
+        mm2(h_acc[2], 1, 2)
+        quantize(w_codes[3], w_scales[3], w_int[3], E5M2X4)
         mm2(h_acc[1], 2, 1)
         mm2(h_acc[3], 2, 3)
-        quantize(e_codes[3], e_scales[3], e_int[3], E4M3X4)
-        mm2(h_acc[0], 2, 0)
-        quantize(w_codes[3], w_scales[3], w_int[3], E5M2X4)
+        mm2(h_acc[3], 3, 3)
         mm2(h_acc[1], 3, 1)
+        finish(h_acc[3], 3)
+        mm2(h_acc[2], 2, 2)
         mm2(h_acc[2], 3, 2)
         finish(h_acc[1], 1)
-        mm2(h_acc[0], 3, 0)
-        mm2(h_acc[3], 3, 3)
+        mm2(h_acc[0], 1, 0)
+        mm2(h_acc[0], 2, 0)
         finish(h_acc[2], 2)
-        finish(h_acc[3], 3)
+        mm2(h_acc[0], 3, 0)
         finish(h_acc[0], 0)

@@ -18,15 +18,14 @@ MULT = mybir.AluOpType.mult
 ADD = mybir.AluOpType.add
 
 P = 128
-GROUPS = K // 512
-
-
-def interleaved(tile_ap):
-    return tile_ap.rearrange("p (c i) t -> p c t i", i=4)
-
-
-def by_row(tile_ap):
-    return tile_ap.rearrange("p t (c i) -> p c t i", i=4)
+SLOTS = 4
+GROUPS = range(K // (P * SLOTS))
+RUN_GROUPS = GROUPS[1:]
+HALF = K // 2
+BANKS = 8
+EARLY_TILES = 6
+V_COLS_BY_PASS = (320, 192, 192, 192)
+V_COLS = 192
 
 
 def tile_scaled_block_projection_s9_kernel(tc, dirs, a_words, a_scales, pot, rho, out):
@@ -39,327 +38,253 @@ def tile_scaled_block_projection_s9_kernel(tc, dirs, a_words, a_scales, pot, rho
         def sb(shape, dtype, name):
             return keep.tile(shape, dtype, name=name, tag=name, align_bytes=64)
 
-        def bank(i, dtype=F32, cols=512):
-            return psum.tile([P, cols], dtype, name="bank%d" % i, tag="bank%d" % i)
+        def bank(i, shape=(P, B), dtype=F32):
+            return psum.tile(list(shape), dtype, name="bank%d" % i, tag="bank%d" % i)
 
-        G = range(GROUPS)
-        REGROUPED = (1, 2)
-        MOVED = (0, 3)
-        d_raw = [sb([P, 4, B], BF16, "d_raw%d" % g) for g in G]
-        d_int = [sb([P, B, 4], BF16, "d_int%d" % g) for g in G]
-        d_codes = [sb([P, B], U32, "d_codes%d" % g) for g in G]
-        d_scales = [sb([P, B], U8, "d_scales%d" % g) for g in G]
-        d_flat = {g: sb([P, 4, B], BF16, "d_flat%d" % g) for g in REGROUPED}
-        w_flat = {g: sb([P, 4, B], BF16, "w_flat%d" % g) for g in REGROUPED}
-        w_raw = [sb([P, 4, B], BF16, "w_raw%d" % g) for g in G]
-        w_int = [sb([P, B, 4], BF16, "w_int%d" % g) for g in G]
-        w_codes = [sb([P, B], U32, "w_codes%d" % g) for g in G]
-        w_scales = [sb([P, B], U8, "w_scales%d" % g) for g in G]
-        a_raw = [sb([P, 2 * K], U8, "a_raw%d" % g) for g in G]
-        s_raw = [sb([P, GROUPS, K // 2], U8, "s_raw%d" % h) for h in range(2)]
-        a_moved = {(g, j): sb([P, 1024], U8, "a_moved%d_%d" % (g, j)) for g in G for j in MOVED}
-        s_moved = {j: sb([P, GROUPS, B], U8, "s_moved%d" % j) for j in MOVED}
-        pot_moved = {j: sb([P, 4], BF16, "pot_moved%d" % j) for j in MOVED}
-        rows = sb([P, P], BF16, "rows")
+        d_raw = [sb([P, SLOTS, B], BF16, "d_raw%d" % g) for g in GROUPS]
+        d_mix = [sb([P, B, SLOTS], BF16, "d_mix%d" % g) for g in GROUPS]
+        d_codes = [sb([P, B], U32, "d_codes%d" % g) for g in GROUPS]
+        d_scales = [sb([P, B], U8, "d_scales%d" % g) for g in GROUPS]
+        e_raw = d_raw[:1] + [sb([P, SLOTS, B], BF16, "e_raw%d" % j) for j in RUN_GROUPS]
+        e_mix = d_mix[:1] + [sb([P, B, SLOTS], BF16, "e_mix%d" % j) for j in RUN_GROUPS]
+        e_codes = d_codes[:1] + [sb([P, B], U32, "e_codes%d" % j) for j in RUN_GROUPS]
+        e_scales = d_scales[:1] + [sb([P, B], U8, "e_scales%d" % j) for j in RUN_GROUPS]
+        w_raw = [sb([P, SLOTS, B], BF16, "w_raw%d" % j) for j in GROUPS]
+        w_mix = [sb([P, B, SLOTS], BF16, "w_mix%d" % j) for j in GROUPS]
+        w_codes = [sb([P, B], U32, "w_codes%d" % j) for j in GROUPS]
+        w_scales = [sb([P, B], U8, "w_scales%d" % j) for j in GROUPS]
+        a_raw = [sb([P, 2 * K], U8, "a_raw%d" % g) for g in GROUPS]
+        a_moved = [[sb([P, 2 * B], U8, "a_moved%d_%d" % (g, j)) for j in (0, 1)] for g in GROUPS]
+        a_late = [sb([P, 2 * HALF], U8, "a_late%d" % g) for g in GROUPS]
+        s_raw = [sb([P, len(GROUPS), HALF], U8, "s_raw%d" % h) for h in (0, 1)]
+        s_moved = [sb([P, len(GROUPS), B], U8, "s_moved%d" % j) for j in (0, 1)]
+        s_late = sb([P, len(GROUPS), HALF], U8, "s_late")
+        rows = sb([P, K // len(GROUPS)], BF16, "rows")
+        rows_straight = sb([P, SLOTS, P], BF16, "rows_straight")
+        rows_runs = sb([P, SLOTS, P], BF16, "rows_runs")
         ident = sb([P, P], BF16, "ident")
-        coef = sb([P, 12], F32, "coef")
+        pot_straight = sb([P, SLOTS], F32, "pot_straight")
+        pot_runs = sb([P, SLOTS, len(GROUPS)], F32, "pot_runs")
+        rho_part = sb([P, B // P], F32, "rho_part")
         rho_all = sb([P, B], BF16, "rho_all")
 
-        def load_scales(h):
+
+        def load_a(g, half):
+            nc.sync.dma_start(
+                out=a_raw[g][:, 2 * HALF * half : 2 * HALF * (half + 1)].bitcast(I32),
+                in_=a_words[g][:, 2 * HALF * half : 2 * HALF * (half + 1)].bitcast(I32),
+            )
+
+        def load_a_scales(half):
             for q in range(4):
                 nc.sync.dma_start(
-                    out=s_raw[h][32 * q : 32 * q + 4, :, :].bitcast(I32),
-                    in_=a_scales[:, 4 * q : 4 * q + 4, 1024 * h : 1024 * (h + 1)]
+                    out=s_raw[half][32 * q : 32 * q + 4, :, :].bitcast(I32),
+                    in_=a_scales[:, 4 * q : 4 * q + 4, HALF * half : HALF * (half + 1)]
                     .rearrange("g r n -> r g n")
                     .bitcast(I32),
                 )
 
-        def load_a(g, lo, hi):
-            nc.sync.dma_start(
-                out=a_raw[g][:, 2 * lo : 2 * hi].bitcast(I32),
-                in_=a_words[g][:, 2 * lo : 2 * hi].bitcast(I32),
-            )
-
         def load_d(g):
-            nc.sync.dma_start(
-                out=d_raw[g][:],
-                in_=dirs[512 * g : 512 * (g + 1), :].rearrange("(p t) b -> p t b", t=4),
-            )
+            rows_of_d = dirs[512 * g : 512 * (g + 1), :]
+            nc.sync.dma_start(out=d_raw[g][:], in_=rows_of_d.rearrange("(p t) b -> p t b", t=SLOTS))
 
-        def load_e(g):
-            nc.sync.dma_start(
-                out=d_flat[g][:],
-                in_=dirs[512 * g : 512 * (g + 1), :].rearrange("(m p) b -> p m b", m=4),
-            )
-
-        def load_rows():
-            for j in MOVED:
-                nc.sync.dma_start(out=pot_moved[j][:], in_=pot[512 * j : 512 * (j + 1)].rearrange("(p t) -> p t", t=4))
-            nc.sync.dma_start(
-                out=rows[0:8, :], in_=pot[512 : 1536].rearrange("(i x) -> i x", x=P)
-            )
-            nc.sync.dma_start(out=rows[8:12, :], in_=rho.rearrange("(m x) -> m x", x=P))
+        def load_e(j):
+            by_r = dirs[512 * j : 512 * (j + 1), :].rearrange("(s t r) b -> r s t b", t=SLOTS, r=4)
+            for r in range(4):
+                nc.sync.dma_start(out=e_raw[j][r:P:4, :, :], in_=by_r[r])
 
         nc.vector.memset(rows[:], 0.0)
-        for h in range(2):
-            nc.vector.memset(s_raw[h][:].rearrange("p g n -> p (g n)").bitcast(I32), 0)
+        for half in (0, 1):
+            nc.vector.memset(s_raw[half][:].rearrange("p g n -> p (g n)").bitcast(I32), 0)
         make_identity(nc, ident[:])
 
-        def v_interleave(dst, src, lo, hi):
-            nc.vector.tensor_copy(out=interleaved(dst[:, lo:hi, :]), in_=by_row(src[:, :, lo:hi]))
+        for g in GROUPS:
+            load_a(g, 0)
+            if g == 0:
+                nc.sync.dma_start(out=rows[0:4, :], in_=pot.rearrange("(j x) -> j x", x=512))
+                nc.sync.dma_start(out=rows[4:5, :], in_=rho.rearrange("(o x) -> o x", o=1))
+            load_d(g)
+            if g == 0:
+                load_a_scales(0)
+        load_e(1)
+        load_a(0, 1)
+        load_a_scales(1)
+        load_e(2)
+        for g in GROUPS[1:]:
+            load_a(g, 1)
+        load_e(3)
+        nc.sync.dma_start(out=rho_all[:], in_=rho.partition_broadcast(P))
 
-        def s_interleave(dst, src, lo, hi):
-            nc.scalar.copy(out=interleaved(dst[:, lo:hi, :]), in_=by_row(src[:, :, lo:hi]))
 
-        def quantize(codes, scales, src, fmt):
+        nc.scalar.copy(out=rows_straight[:], in_=rows[:].rearrange("p (m t) -> p t m", t=SLOTS))
+        nc.scalar.copy(
+            out=rows_runs[:].rearrange("p t (s r) -> p t s r", r=4),
+            in_=rows[:].rearrange("p (s t r) -> p t s r", t=SLOTS, r=4),
+        )
+        turned_pot = bank(6, (P, 2, SLOTS, P), BF16)
+        turned_rho = bank(7, (P, B // P, P), BF16)
+        for t in range(SLOTS):
+            nc.tensor.transpose(turned_pot[:, 0, t, :], rows_straight[:, t, :], ident[:])
+            nc.tensor.transpose(turned_pot[:, 1, t, :], rows_runs[:, t, :], ident[:])
+        for m in range(B // P):
+            nc.tensor.transpose(turned_rho[:, m, :], rows[:, P * m : P * (m + 1)], ident[:])
+
+
+        def interleave(mix, raw, v_cols):
+            for copy, lo, hi in ((nc.vector.tensor_copy, 0, v_cols), (nc.scalar.copy, v_cols, B)):
+                if lo < hi:
+                    copy(
+                        out=mix[:, lo:hi, :].rearrange("p (c i) t -> p c t i", i=4),
+                        in_=raw[:, :, lo:hi].rearrange("p t (c i) -> p c t i", i=4),
+                    )
+
+        def quantize(codes, scales, mix, fmt):
             nc.vector.quantize_mx(
-                out=codes[:].bitcast(fmt), scales=scales[:], in_=src[:].rearrange("p b t -> p (b t)")
+                out=codes[:].bitcast(fmt), scales=scales[:], in_=mix[:].rearrange("p b t -> p (b t)")
             )
 
-        def move_scales(j):
-            h, k = divmod(j, 2)
+        def move_words_straight(g):
             nc.vector.tensor_copy(
-                out=s_moved[j][:].rearrange("p g (t m) -> p g t m", t=4),
-                in_=s_raw[h][:, :, 512 * k : 512 * (k + 1)].rearrange("p g (m t) -> p g t m", t=4),
+                out=a_moved[g][0][:].rearrange("p (t m e) -> p t m e", t=SLOTS, e=2),
+                in_=a_raw[g][:, 0 : 2 * B].rearrange("p (m t e) -> p t m e", t=SLOTS, e=2),
             )
 
-        def move_words(g, j):
+        def move_scales_straight():
             nc.vector.tensor_copy(
-                out=a_moved[g, j][:].rearrange("p (t m e) -> p t m e", t=4, e=2),
-                in_=a_raw[g][:, 1024 * j : 1024 * (j + 1)].rearrange("p (m t e) -> p t m e", t=4, e=2),
+                out=s_moved[0][:].rearrange("p g (t m) -> p g t m", t=SLOTS),
+                in_=s_raw[0][:, :, 0:B].rearrange("p g (m t) -> p g t m", t=SLOTS),
             )
 
-        def mm1(acc, g, i):
-            j, n = divmod(i, 4)
-            if j in MOVED:
-                words = a_moved[g, j][:, 256 * n : 256 * (n + 1)]
-                scales = s_moved[j][:, g, 128 * n : 128 * (n + 1)]
+        def move_words_runs(dst, src):
+            nc.vector.tensor_copy(
+                out=dst.bitcast(I32).rearrange("p (j t s e) -> p j t s e", t=SLOTS, s=P // 4, e=2),
+                in_=src.bitcast(I32).rearrange("p (j s t e) -> p j t s e", t=SLOTS, s=P // 4, e=2),
+            )
+
+        def move_scales_runs(dst, src):
+            nc.vector.tensor_copy(
+                out=dst.bitcast(I32).rearrange("p g (j t s) -> p g j t s", t=SLOTS, s=P // 4),
+                in_=src.bitcast(I32).rearrange("p g (j s t) -> p g j t s", t=SLOTS, s=P // 4),
+            )
+
+        def move_early_words(g):
+            move_words_straight(g)
+            move_words_runs(a_moved[g][1][:], a_raw[g][:, 2 * B : 4 * B])
+
+        def first_product(acc, i, g):
+            j, t = divmod(i, SLOTS)
+            if j < 2:
+                words, scales, c = a_moved[g][j], s_moved[j], P * t
             else:
-                words = a_raw[g][:, 256 * i : 256 * (i + 1)]
-                scales = s_raw[i // 8][:, g, 128 * (i % 8) : 128 * (i % 8 + 1)]
+                words, scales, c = a_late[g], s_late, P * (i - 2 * SLOTS)
             nc.tensor.matmul_mx(
                 out=acc[:],
-                lhsT=words.bitcast(E2M1X4),
-                lhsT_scale=scales,
+                lhsT=words[:, 2 * c : 2 * (c + P)].bitcast(E2M1X4),
+                lhsT_scale=scales[:, g, c : c + P],
                 rhs=d_codes[g][:].bitcast(E4M3X4),
                 rhs_scale=d_scales[g][:],
                 start=(g == 0),
-                stop=(g == GROUPS - 1),
+                stop=(g == len(GROUPS) - 1),
             )
 
-        def combine(acc, i):
-            j, n = divmod(i, 4)
-            if j in MOVED:
-                w, d, v = w_raw[j], d_raw[j], pot_moved[j][:, n : n + 1]
-            else:
-                w, d, v = w_flat[j], d_flat[j], coef[:, i - 4 : i - 3]
+        def add_potential(acc, i):
+            j, t = divmod(i, SLOTS)
             nc.vector.scalar_tensor_tensor(
-                out=w[:, n, :], in0=d[:, n, :], scalar=v, in1=acc[:], op0=MULT, op1=ADD
+                out=w_raw[j][:, t, :],
+                in0=e_raw[j][:, t, :],
+                scalar=pot_straight[:, t : t + 1] if j == 0 else pot_runs[:, t, j : j + 1],
+                in1=acc[:],
+                op0=MULT,
+                op1=ADD,
             )
 
-        def regroup(i):
-            j, n = divmod(i, 4)
-            for t in range(4):
-                nc.sync.dma_start(out=w_raw[j][32 * n : 32 * n + 32, t, :], in_=w_flat[j][t : 128 : 4, n, :])
-
-        def mm2(acc, j, m):
-            cols = slice(128 * m, 128 * (m + 1))
+        def second_product(acc, m, j):
+            cols = slice(P * m, P * (m + 1))
             nc.tensor.matmul_mx(
                 out=acc[:],
-                lhsT=d_codes[j][:, cols].bitcast(E4M3X4),
-                lhsT_scale=d_scales[j][:, cols],
+                lhsT=e_codes[j][:, cols].bitcast(E4M3X4),
+                lhsT_scale=e_scales[j][:, cols],
                 rhs=w_codes[j][:].bitcast(E5M2X4),
                 rhs_scale=w_scales[j][:],
                 start=(j == 0),
-                stop=(j == GROUPS - 1),
+                stop=(j == len(GROUPS) - 1),
             )
 
-        def finish(acc_m, m):
+        def finish(acc, m):
             res = sb([P, B], F32, "res%d" % m)
             nc.vector.scalar_tensor_tensor(
-                out=res[:], in0=acc_m[:], scalar=coef[:, 8 + m : 9 + m], in1=rho_all[:], op0=MULT, op1=MULT,
+                out=res[:], in0=acc[:], scalar=rho_part[:, m : m + 1], in1=rho_all[:], op0=MULT, op1=MULT
             )
-            nc.sync.dma_start(out=out[128 * m : 128 * (m + 1), :], in_=res[:])
+            nc.sync.dma_start(out=out[P * m : P * (m + 1), :], in_=res[:])
 
-        turned = bank(7, BF16, P)
-        acc = [None] * 16
-        h_acc = [None] * 4
-        load_d(0)
-        load_scales(0)
-        load_a(0, 0, 1024)
-        load_rows()
-        load_d(1)
-        s_interleave(d_int[0], d_raw[0], 0, 512)
-        load_d(2)
-        load_d(3)
-        load_a(1, 0, 1024)
-        load_a(2, 0, 1024)
-        move_scales(0)
-        load_a(3, 1024, 2048)
-        nc.tensor.transpose(turned[:], rows[:], ident[:])
-        load_a(0, 1024, 2048)
-        load_a(3, 0, 1024)
-        move_words(0, 0)
-        nc.scalar.copy(out=coef[:], in_=turned[:, 0:12])
-        quantize(d_codes[0], d_scales[0], d_int[0], E4M3X4)
-        load_e(1)
-        s_interleave(d_int[1], d_raw[1], 192, 512)
-        v_interleave(d_int[1], d_raw[1], 0, 192)
-        acc[1] = bank(1)
-        mm1(acc[1], 0, 1)
-        acc[3] = bank(3)
-        mm1(acc[3], 0, 3)
-        load_scales(1)
-        v_interleave(d_int[2], d_raw[2], 0, 256)
-        acc[0] = bank(0)
-        mm1(acc[0], 0, 0)
-        s_interleave(d_int[2], d_raw[2], 256, 512)
-        acc[4] = bank(4)
-        mm1(acc[4], 0, 4)
-        quantize(d_codes[1], d_scales[1], d_int[1], E4M3X4)
-        acc[2] = bank(2)
-        mm1(acc[2], 0, 2)
-        v_interleave(d_int[3], d_raw[3], 0, 64)
-        acc[6] = bank(6)
-        mm1(acc[6], 0, 6)
-        s_interleave(d_int[3], d_raw[3], 64, 512)
-        quantize(d_codes[2], d_scales[2], d_int[2], E4M3X4)
-        acc[7] = bank(7)
-        mm1(acc[7], 0, 7)
-        mm1(acc[7], 1, 7)
-        move_words(1, 0)
-        mm1(acc[4], 1, 4)
-        mm1(acc[7], 2, 7)
-        mm1(acc[4], 2, 4)
-        move_words(2, 0)
-        mm1(acc[2], 1, 2)
-        load_e(2)
-        mm1(acc[3], 1, 3)
-        move_words(3, 3)
-        mm1(acc[3], 2, 3)
-        load_a(2, 1024, 2048)
-        mm1(acc[0], 1, 0)
-        quantize(d_codes[3], d_scales[3], d_int[3], E4M3X4)
-        mm1(acc[0], 2, 0)
-        mm1(acc[2], 2, 2)
-        load_a(1, 1024, 2048)
-        mm1(acc[1], 1, 1)
-        move_words(3, 0)
-        mm1(acc[7], 3, 7)
-        mm1(acc[1], 2, 1)
-        move_words(0, 3)
-        mm1(acc[2], 3, 2)
-        mm1(acc[0], 3, 0)
-        combine(acc[2], 2)
-        mm1(acc[3], 3, 3)
-        nc.sync.dma_start(out=rho_all[:], in_=rho.partition_broadcast(P))
-        mm1(acc[1], 3, 1)
-        mm1(acc[4], 3, 4)
-        combine(acc[3], 3)
-        acc[5] = bank(5)
-        mm1(acc[5], 0, 5)
-        mm1(acc[5], 1, 5)
-        combine(acc[0], 0)
-        mm1(acc[5], 2, 5)
-        mm1(acc[5], 3, 5)
-        combine(acc[1], 1)
-        acc[11] = bank(3)
-        mm1(acc[11], 0, 11)
-        acc[10] = bank(2)
-        mm1(acc[10], 0, 10)
-        combine(acc[7], 7)
-        acc[9] = bank(1)
-        mm1(acc[9], 0, 9)
-        s_interleave(w_int[0], w_raw[0], 0, 512)
-        acc[8] = bank(0)
-        mm1(acc[8], 0, 8)
-        combine(acc[5], 5)
-        mm1(acc[6], 1, 6)
-        regroup(7)
-        mm1(acc[6], 2, 6)
-        mm1(acc[6], 3, 6)
-        combine(acc[4], 4)
-        regroup(5)
-        combine(acc[6], 6)
-        mm1(acc[10], 1, 10)
-        mm1(acc[8], 1, 8)
-        move_words(1, 3)
-        mm1(acc[11], 1, 11)
-        regroup(4)
-        mm1(acc[11], 2, 11)
-        move_scales(3)
-        mm1(acc[11], 3, 11)
-        regroup(6)
-        mm1(acc[10], 2, 10)
-        mm1(acc[10], 3, 10)
-        mm1(acc[8], 2, 8)
-        mm1(acc[8], 3, 8)
-        combine(acc[11], 11)
-        acc[14] = bank(6)
-        mm1(acc[14], 0, 14)
-        mm1(acc[14], 1, 14)
-        combine(acc[8], 8)
-        regroup(11)
-        acc[12] = bank(4)
-        mm1(acc[12], 0, 12)
-        mm1(acc[12], 1, 12)
-        combine(acc[10], 10)
-        mm1(acc[9], 1, 9)
-        regroup(8)
-        mm1(acc[9], 2, 9)
-        move_words(2, 3)
-        mm1(acc[9], 3, 9)
-        s_interleave(w_int[1], w_raw[1], 0, 512)
-        acc[13] = bank(5)
-        mm1(acc[13], 0, 13)
-        mm1(acc[13], 1, 13)
-        combine(acc[9], 9)
-        regroup(10)
-        mm1(acc[14], 2, 14)
-        mm1(acc[14], 3, 14)
-        quantize(w_codes[0], w_scales[0], w_int[0], E5M2X4)
-        regroup(9)
-        mm1(acc[13], 2, 13)
-        mm1(acc[13], 3, 13)
-        combine(acc[14], 14)
-        mm1(acc[12], 2, 12)
-        mm1(acc[12], 3, 12)
-        combine(acc[13], 13)
-        acc[15] = bank(7)
-        mm1(acc[15], 0, 15)
-        mm1(acc[15], 1, 15)
-        mm1(acc[15], 2, 15)
-        combine(acc[12], 12)
-        mm1(acc[15], 3, 15)
-        h_acc[0] = bank(0)
-        mm2(h_acc[0], 0, 0)
-        combine(acc[15], 15)
-        h_acc[2] = bank(2)
-        mm2(h_acc[2], 0, 2)
-        s_interleave(w_int[2], w_raw[2], 128, 512)
-        h_acc[1] = bank(1)
-        mm2(h_acc[1], 0, 1)
-        v_interleave(w_int[2], w_raw[2], 0, 128)
-        h_acc[3] = bank(3)
-        mm2(h_acc[3], 0, 3)
-        v_interleave(w_int[3], w_raw[3], 0, 320)
-        quantize(w_codes[1], w_scales[1], w_int[1], E5M2X4)
-        s_interleave(w_int[3], w_raw[3], 320, 512)
-        quantize(w_codes[2], w_scales[2], w_int[2], E5M2X4)
-        mm2(h_acc[1], 1, 1)
-        mm2(h_acc[3], 1, 3)
-        mm2(h_acc[2], 1, 2)
-        quantize(w_codes[3], w_scales[3], w_int[3], E5M2X4)
-        mm2(h_acc[1], 2, 1)
-        mm2(h_acc[3], 2, 3)
-        mm2(h_acc[3], 3, 3)
-        mm2(h_acc[1], 3, 1)
-        finish(h_acc[3], 3)
-        mm2(h_acc[2], 2, 2)
-        mm2(h_acc[2], 3, 2)
-        finish(h_acc[1], 1)
-        mm2(h_acc[0], 1, 0)
-        mm2(h_acc[0], 2, 0)
-        finish(h_acc[2], 2)
-        mm2(h_acc[0], 3, 0)
-        finish(h_acc[0], 0)
+
+        acc = [bank(i) for i in range(EARLY_TILES)]
+        move_early_words(0)
+        for g in GROUPS:
+            interleave(d_mix[g], d_raw[g], V_COLS_BY_PASS[g])
+            if 0 < g < len(GROUPS) - 1:
+                move_early_words(g + 1)
+            if g == len(GROUPS) - 1:
+                move_words_runs(a_late[0][:], a_raw[0][:, 2 * HALF :])
+            quantize(d_codes[g], d_scales[g], d_mix[g], E4M3X4)
+            if g == 0:
+                move_scales_straight()
+                move_scales_runs(s_moved[1][:], s_raw[0][:, :, B:])
+                move_early_words(1)
+            for i in range(EARLY_TILES):
+                first_product(acc[i], i, g)
+        nc.scalar.copy(out=pot_straight[:], in_=turned_pot[:, 0, :, 0])
+        nc.scalar.copy(out=pot_runs[:], in_=turned_pot[:, 1, :, 0 : len(GROUPS)])
+        nc.scalar.copy(out=rho_part[:], in_=turned_rho[:, :, 4])
+        for i in range(EARLY_TILES, BANKS):
+            acc.append(bank(i))
+            for g in GROUPS:
+                first_product(acc[i], i, g)
+
+
+        interleave(e_mix[1], e_raw[1], 0)
+        interleave(e_mix[2], e_raw[2], 0)
+        for i in range(SLOTS):
+            add_potential(acc[i], i)
+        interleave(w_mix[0], w_raw[0], 0)
+        move_scales_runs(s_late[:], s_raw[1][:])
+        for g in GROUPS[1:]:
+            move_words_runs(a_late[g][:], a_raw[g][:, 2 * HALF :])
+            add_potential(acc[SLOTS + g - 1], SLOTS + g - 1)
+        add_potential(acc[7], 7)
+
+
+        acc += [bank(i - BANKS) for i in range(8, 12)]
+        for g in GROUPS:
+            for i in range(8, 12):
+                first_product(acc[i], i, g)
+        interleave(e_mix[3], e_raw[3], 0)
+        interleave(w_mix[1], w_raw[1], 0)
+        quantize(w_codes[0], w_scales[0], w_mix[0], E5M2X4)
+        quantize(e_codes[1], e_scales[1], e_mix[1], E4M3X4)
+        for i in range(12, 16):
+            acc.append(bank(i - BANKS))
+            for g in GROUPS:
+                first_product(acc[i], i, g)
+        for i in range(8, 12):
+            add_potential(acc[i], i)
+        interleave(w_mix[2], w_raw[2], 0)
+        quantize(e_codes[2], e_scales[2], e_mix[2], E4M3X4)
+        h_acc = [bank(m) for m in range(4)]
+        for m in range(4):
+            second_product(h_acc[m], m, 0)
+        for i in range(12, 16):
+            add_potential(acc[i], i)
+        quantize(w_codes[1], w_scales[1], w_mix[1], E5M2X4)
+        for m in range(4):
+            second_product(h_acc[m], m, 1)
+        interleave(w_mix[3], w_raw[3], V_COLS)
+        quantize(w_codes[2], w_scales[2], w_mix[2], E5M2X4)
+        quantize(e_codes[3], e_scales[3], e_mix[3], E4M3X4)
+        for m in range(4):
+            second_product(h_acc[m], m, 2)
+        quantize(w_codes[3], w_scales[3], w_mix[3], E5M2X4)
+        for m in range(4):
+            second_product(h_acc[m], m, 3)
+        for m in range(4):
+            finish(h_acc[m], m)

from contextlib import ExitStack

import concourse.mybir as mybir
from concourse.masks import make_identity

K, B = 2048, 512
FLOPS = 2 * K * K * B + 2 * K * B * B

F32 = mybir.dt.float32
BF16 = mybir.dt.bfloat16
U32 = mybir.dt.uint32
I32 = mybir.dt.int32
U8 = mybir.dt.uint8
E4M3X4 = mybir.dt.float8_e4m3fn_x4
E5M2X4 = mybir.dt.float8_e5m2_x4
E2M1X4 = mybir.dt.float4_e2m1fn_x4
MULT = mybir.AluOpType.mult
ADD = mybir.AluOpType.add

P = 128
SLOTS = 4
GROUPS = range(K // (P * SLOTS))
RUN_GROUPS = GROUPS[1:]
HALF = K // 2
BANKS = 8
EARLY_TILES = 6
V_COLS_BY_PASS = (320, 192, 192, 192)
V_COLS = 192


def tile_scaled_block_projection_s9_kernel(tc, dirs, a_words, a_scales, pot, rho, out):
    nc = tc.nc
    with ExitStack() as ctx:
        keep = ctx.enter_context(tc.tile_pool(name="keep", bufs=1))
        psum = ctx.enter_context(tc.psum_pool(name="psum", bufs=1))
        ctx.enter_context(tc.manual_schedule())

        def sb(shape, dtype, name):
            return keep.tile(shape, dtype, name=name, tag=name, align_bytes=64)

        def bank(i, shape=(P, B), dtype=F32):
            return psum.tile(list(shape), dtype, name="bank%d" % i, tag="bank%d" % i)

        d_raw = [sb([P, SLOTS, B], BF16, "d_raw%d" % g) for g in GROUPS]
        d_mix = [sb([P, B, SLOTS], BF16, "d_mix%d" % g) for g in GROUPS]
        d_codes = [sb([P, B], U32, "d_codes%d" % g) for g in GROUPS]
        d_scales = [sb([P, B], U8, "d_scales%d" % g) for g in GROUPS]
        e_raw = d_raw[:1] + [sb([P, SLOTS, B], BF16, "e_raw%d" % j) for j in RUN_GROUPS]
        e_mix = d_mix[:1] + [sb([P, B, SLOTS], BF16, "e_mix%d" % j) for j in RUN_GROUPS]
        e_codes = d_codes[:1] + [sb([P, B], U32, "e_codes%d" % j) for j in RUN_GROUPS]
        e_scales = d_scales[:1] + [sb([P, B], U8, "e_scales%d" % j) for j in RUN_GROUPS]
        w_raw = [sb([P, SLOTS, B], BF16, "w_raw%d" % j) for j in GROUPS]
        w_mix = [sb([P, B, SLOTS], BF16, "w_mix%d" % j) for j in GROUPS]
        w_codes = [sb([P, B], U32, "w_codes%d" % j) for j in GROUPS]
        w_scales = [sb([P, B], U8, "w_scales%d" % j) for j in GROUPS]
        a_raw = [sb([P, 2 * K], U8, "a_raw%d" % g) for g in GROUPS]
        a_moved = [[sb([P, 2 * B], U8, "a_moved%d_%d" % (g, j)) for j in (0, 1)] for g in GROUPS]
        a_late = [sb([P, 2 * HALF], U8, "a_late%d" % g) for g in GROUPS]
        s_raw = [sb([P, len(GROUPS), HALF], U8, "s_raw%d" % h) for h in (0, 1)]
        s_moved = [sb([P, len(GROUPS), B], U8, "s_moved%d" % j) for j in (0, 1)]
        s_late = sb([P, len(GROUPS), HALF], U8, "s_late")
        rows = sb([P, K // len(GROUPS)], BF16, "rows")
        rows_straight = sb([P, SLOTS, P], BF16, "rows_straight")
        rows_runs = sb([P, SLOTS, P], BF16, "rows_runs")
        ident = sb([P, P], BF16, "ident")
        pot_straight = sb([P, SLOTS], F32, "pot_straight")
        pot_runs = sb([P, SLOTS, len(GROUPS)], F32, "pot_runs")
        rho_part = sb([P, B // P], F32, "rho_part")
        rho_all = sb([P, B], BF16, "rho_all")


        def load_a(g, half):
            nc.sync.dma_start(
                out=a_raw[g][:, 2 * HALF * half : 2 * HALF * (half + 1)].bitcast(I32),
                in_=a_words[g][:, 2 * HALF * half : 2 * HALF * (half + 1)].bitcast(I32),
            )

        def load_a_scales(half):
            for q in range(4):
                nc.sync.dma_start(
                    out=s_raw[half][32 * q : 32 * q + 4, :, :].bitcast(I32),
                    in_=a_scales[:, 4 * q : 4 * q + 4, HALF * half : HALF * (half + 1)]
                    .rearrange("g r n -> r g n")
                    .bitcast(I32),
                )

        def load_d(g):
            rows_of_d = dirs[512 * g : 512 * (g + 1), :]
            nc.sync.dma_start(out=d_raw[g][:], in_=rows_of_d.rearrange("(p t) b -> p t b", t=SLOTS))

        def load_e(j):
            by_r = dirs[512 * j : 512 * (j + 1), :].rearrange("(s t r) b -> r s t b", t=SLOTS, r=4)
            for r in range(4):
                nc.sync.dma_start(out=e_raw[j][r:P:4, :, :], in_=by_r[r])

        nc.vector.memset(rows[:], 0.0)
        for half in (0, 1):
            nc.vector.memset(s_raw[half][:].rearrange("p g n -> p (g n)").bitcast(I32), 0)
        make_identity(nc, ident[:])

        for g in GROUPS:
            load_a(g, 0)
            if g == 0:
                nc.sync.dma_start(out=rows[0:4, :], in_=pot.rearrange("(j x) -> j x", x=512))
                nc.sync.dma_start(out=rows[4:5, :], in_=rho.rearrange("(o x) -> o x", o=1))
            load_d(g)
            if g == 0:
                load_a_scales(0)
        load_e(1)
        load_a(0, 1)
        load_a_scales(1)
        load_e(2)
        for g in GROUPS[1:]:
            load_a(g, 1)
        load_e(3)
        nc.sync.dma_start(out=rho_all[:], in_=rho.partition_broadcast(P))


        nc.scalar.copy(out=rows_straight[:], in_=rows[:].rearrange("p (m t) -> p t m", t=SLOTS))
        nc.scalar.copy(
            out=rows_runs[:].rearrange("p t (s r) -> p t s r", r=4),
            in_=rows[:].rearrange("p (s t r) -> p t s r", t=SLOTS, r=4),
        )
        turned_pot = bank(6, (P, 2, SLOTS, P), BF16)
        turned_rho = bank(7, (P, B // P, P), BF16)
        for t in range(SLOTS):
            nc.tensor.transpose(turned_pot[:, 0, t, :], rows_straight[:, t, :], ident[:])
            nc.tensor.transpose(turned_pot[:, 1, t, :], rows_runs[:, t, :], ident[:])
        for m in range(B // P):
            nc.tensor.transpose(turned_rho[:, m, :], rows[:, P * m : P * (m + 1)], ident[:])


        def interleave(mix, raw, v_cols):
            for copy, lo, hi in ((nc.vector.tensor_copy, 0, v_cols), (nc.scalar.copy, v_cols, B)):
                if lo < hi:
                    copy(
                        out=mix[:, lo:hi, :].rearrange("p (c i) t -> p c t i", i=4),
                        in_=raw[:, :, lo:hi].rearrange("p t (c i) -> p c t i", i=4),
                    )

        def quantize(codes, scales, mix, fmt):
            nc.vector.quantize_mx(
                out=codes[:].bitcast(fmt), scales=scales[:], in_=mix[:].rearrange("p b t -> p (b t)")
            )

        def move_words_straight(g):
            nc.vector.tensor_copy(
                out=a_moved[g][0][:].rearrange("p (t m e) -> p t m e", t=SLOTS, e=2),
                in_=a_raw[g][:, 0 : 2 * B].rearrange("p (m t e) -> p t m e", t=SLOTS, e=2),
            )

        def move_scales_straight():
            nc.vector.tensor_copy(
                out=s_moved[0][:].rearrange("p g (t m) -> p g t m", t=SLOTS),
                in_=s_raw[0][:, :, 0:B].rearrange("p g (m t) -> p g t m", t=SLOTS),
            )

        def move_words_runs(dst, src):
            nc.vector.tensor_copy(
                out=dst.bitcast(I32).rearrange("p (j t s e) -> p j t s e", t=SLOTS, s=P // 4, e=2),
                in_=src.bitcast(I32).rearrange("p (j s t e) -> p j t s e", t=SLOTS, s=P // 4, e=2),
            )

        def move_scales_runs(dst, src):
            nc.vector.tensor_copy(
                out=dst.bitcast(I32).rearrange("p g (j t s) -> p g j t s", t=SLOTS, s=P // 4),
                in_=src.bitcast(I32).rearrange("p g (j s t) -> p g j t s", t=SLOTS, s=P // 4),
            )

        def move_early_words(g):
            move_words_straight(g)
            move_words_runs(a_moved[g][1][:], a_raw[g][:, 2 * B : 4 * B])

        def first_product(acc, i, g):
            j, t = divmod(i, SLOTS)
            if j < 2:
                words, scales, c = a_moved[g][j], s_moved[j], P * t
            else:
                words, scales, c = a_late[g], s_late, P * (i - 2 * SLOTS)
            nc.tensor.matmul_mx(
                out=acc[:],
                lhsT=words[:, 2 * c : 2 * (c + P)].bitcast(E2M1X4),
                lhsT_scale=scales[:, g, c : c + P],
                rhs=d_codes[g][:].bitcast(E4M3X4),
                rhs_scale=d_scales[g][:],
                start=(g == 0),
                stop=(g == len(GROUPS) - 1),
            )

        def add_potential(acc, i):
            j, t = divmod(i, SLOTS)
            nc.vector.scalar_tensor_tensor(
                out=w_raw[j][:, t, :],
                in0=e_raw[j][:, t, :],
                scalar=pot_straight[:, t : t + 1] if j == 0 else pot_runs[:, t, j : j + 1],
                in1=acc[:],
                op0=MULT,
                op1=ADD,
            )

        def second_product(acc, m, j):
            cols = slice(P * m, P * (m + 1))
            nc.tensor.matmul_mx(
                out=acc[:],
                lhsT=e_codes[j][:, cols].bitcast(E4M3X4),
                lhsT_scale=e_scales[j][:, cols],
                rhs=w_codes[j][:].bitcast(E5M2X4),
                rhs_scale=w_scales[j][:],
                start=(j == 0),
                stop=(j == len(GROUPS) - 1),
            )

        def finish(acc, m):
            res = sb([P, B], F32, "res%d" % m)
            nc.vector.scalar_tensor_tensor(
                out=res[:], in0=acc[:], scalar=rho_part[:, m : m + 1], in1=rho_all[:], op0=MULT, op1=MULT
            )
            nc.sync.dma_start(out=out[P * m : P * (m + 1), :], in_=res[:])


        acc = [bank(i) for i in range(EARLY_TILES)]
        move_early_words(0)
        for g in GROUPS:
            interleave(d_mix[g], d_raw[g], V_COLS_BY_PASS[g])
            if 0 < g < len(GROUPS) - 1:
                move_early_words(g + 1)
            if g == len(GROUPS) - 1:
                move_words_runs(a_late[0][:], a_raw[0][:, 2 * HALF :])
            quantize(d_codes[g], d_scales[g], d_mix[g], E4M3X4)
            if g == 0:
                move_scales_straight()
                move_scales_runs(s_moved[1][:], s_raw[0][:, :, B:])
                move_early_words(1)
            for i in range(EARLY_TILES):
                first_product(acc[i], i, g)
        nc.scalar.copy(out=pot_straight[:], in_=turned_pot[:, 0, :, 0])
        nc.scalar.copy(out=pot_runs[:], in_=turned_pot[:, 1, :, 0 : len(GROUPS)])
        nc.scalar.copy(out=rho_part[:], in_=turned_rho[:, :, 4])
        for i in range(EARLY_TILES, BANKS):
            acc.append(bank(i))
            for g in GROUPS:
                first_product(acc[i], i, g)


        interleave(e_mix[1], e_raw[1], 0)
        interleave(e_mix[2], e_raw[2], 0)
        for i in range(SLOTS):
            add_potential(acc[i], i)
        interleave(w_mix[0], w_raw[0], 0)
        move_scales_runs(s_late[:], s_raw[1][:])
        for g in GROUPS[1:]:
            move_words_runs(a_late[g][:], a_raw[g][:, 2 * HALF :])
            add_potential(acc[SLOTS + g - 1], SLOTS + g - 1)
        add_potential(acc[7], 7)


        acc += [bank(i - BANKS) for i in range(8, 12)]
        for g in GROUPS:
            for i in range(8, 12):
                first_product(acc[i], i, g)
        interleave(e_mix[3], e_raw[3], 0)
        interleave(w_mix[1], w_raw[1], 0)
        quantize(w_codes[0], w_scales[0], w_mix[0], E5M2X4)
        quantize(e_codes[1], e_scales[1], e_mix[1], E4M3X4)
        for i in range(12, 16):
            acc.append(bank(i - BANKS))
            for g in GROUPS:
                first_product(acc[i], i, g)
        for i in range(8, 12):
            add_potential(acc[i], i)
        interleave(w_mix[2], w_raw[2], 0)
        quantize(e_codes[2], e_scales[2], e_mix[2], E4M3X4)
        h_acc = [bank(m) for m in range(4)]
        for m in range(4):
            second_product(h_acc[m], m, 0)
        for i in range(12, 16):
            add_potential(acc[i], i)
        quantize(w_codes[1], w_scales[1], w_mix[1], E5M2X4)
        for m in range(4):
            second_product(h_acc[m], m, 1)
        interleave(w_mix[3], w_raw[3], V_COLS)
        quantize(w_codes[2], w_scales[2], w_mix[2], E5M2X4)
        quantize(e_codes[3], e_scales[3], e_mix[3], E4M3X4)
        for m in range(4):
            second_product(h_acc[m], m, 2)
        quantize(w_codes[3], w_scales[3], w_mix[3], E5M2X4)
        for m in range(4):
            second_product(h_acc[m], m, 3)
        for m in range(4):
            finish(h_acc[m], m)
